import numpy as np, ml_dtypes
CORES = [40,64,80,88,96,104,120,144]
N = 8
import mx_ref
BF = ml_dtypes.bfloat16
def gentries(a):
    return np.ascontiguousarray(a.reshape(8, 16, -1).transpose(0, 2, 1)).reshape(8, -1)
def gtable(e):
    e = np.asarray(e); return np.ascontiguousarray(e.reshape(8, -1, 16).transpose(0, 2, 1)).reshape(128, -1).astype(np.int32)
def gcols(t, e):
    v = np.concatenate([t.reshape(8, 16, -1, 4), np.zeros((8, 16, 1, 4), BF)], axis=2)
    return np.ascontiguousarray(np.stack([v[g][:, e[g]] for g in range(8)])).reshape(128, -1)
def tile(rs):
    return np.stack(rs, axis=2).reshape(128, -1).astype(BF)
def pick(q, e):
    c = np.concatenate([q[0].reshape(128, -1, 4), np.zeros((128, 1, 4), np.uint8)], axis=1); s = np.concatenate([q[1], np.ones((16, 1), np.uint8)], axis=1)
    return (np.ascontiguousarray(c[:, e].reshape(128, -1)), np.ascontiguousarray(s[:, e]))
def join(*qs):
    return (np.concatenate([q[0] for q in qs], axis=1), np.concatenate([q[1] for q in qs], axis=1))
def put(q, e, v):
    c, s = q[0].reshape(128, -1, 4).copy(), q[1].copy(); c[:, e] = v[0].reshape(128, -1, 4); s[:, e] = v[1]
    return (c.reshape(128, -1), s)
def pk(c, s):
    return (np.ascontiguousarray(c), mx_ref.live(s))
def emit(q):
    return q[0], q[1]
def packed(v, rng):
    q = [mx_ref.quantize(np.ascontiguousarray(v[r])) for r in range(N)]
    return np.stack([a for a, b in q]), np.stack([mx_ref.plane(b, rng) for a, b in q])
def values_of_codes():
    e, c = np.zeros((128, 128, 4), np.float32), np.zeros((128, 2, 4), np.uint8)
    e[np.arange(128), np.arange(128), 0] = 1
    c[:127, :, 0] = np.arange(256).reshape(2, 128).T[:127]
    return mx_ref.matmul(mx_ref.quantize(e.reshape(128, 512).astype(BF)), (c.reshape(128, 8), np.full((16, 2), 127, np.uint8))).T.reshape(-1).astype(np.float64)
CODE_VALUE, SCALE_VALUE = values_of_codes(), 2.0 ** (np.arange(256) - 127.0)
def decode(q):
    return (CODE_VALUE[q[0]].reshape(16, 8, -1, 4) * SCALE_VALUE[q[1]][:, None, :, None] + 0.0).reshape(128, -1).astype(np.float32)
def f(rng, *shape):
    return mx_ref.flush((rng.standard_normal(shape, dtype=np.float32) * np.exp2(rng.integers(-2, 3, shape[:-1] + (1,)))).astype(BF))
def wide(rng, *shape, cols=0):
    v = rng.standard_normal(shape, dtype=np.float32) * np.exp2(rng.integers(-12, 13, shape)).astype(np.float32)
    if cols: v *= np.repeat(np.exp2(rng.integers(-cols, cols + 1, shape[:-2] + (1, shape[-1] // 4))) * (rng.random(shape[:-2] + (1, shape[-1] // 4)) > 0.0625), 4, axis=-1).astype(np.float32)
    return mx_ref.flush(v.astype(BF))
C = 352
STEP = [1, 2, 4]
def big(v):
    v = v.astype(np.float32)
    v[np.abs(v) < np.float32(2.0 ** -16)] = 0
    return v.astype(BF)
def numbers_of(rng):
    return {"x": big(f(rng, N, 128, 4 * C)), "u": np.array(f(rng, N, 128, 512)), "v": np.array(f(rng, N, 128, 512))}
def stored(k, t):
    return {"gl": np.stack([gtable(k[r]) for r in range(N)]), "ht": np.stack([gtable(t[r]) for r in range(N)])}
def lists(rng):
    e = np.tile(np.arange(C), (N, 8, 1))
    k = np.stack([rng.permuted(e, axis=2), rng.permuted(e, axis=2)], axis=3).reshape(N, 8, 2 * C)
    return stored(k, rng.integers(0, C, (N, 8, C)))
def layers(rng):
    return big(f(rng, N, 128, 2048)).reshape(N, 8, 16, 4, 8, 16, 4)
def weights(rng, w):
    c, p = packed(np.ascontiguousarray(w).reshape(N, 128, 2048), rng)
    return {"wc": c, "ws": p}
def setup_inputs(rng):
    return {**numbers_of(rng), **lists(rng), **weights(rng, layers(rng))}
def setup_inputs_ties(rng):
    d = numbers_of(rng)
    o = rng.permutation(N)
    k = rng.integers(-1, 2, (N, 8, C)).astype(np.float32)
    k[o[1]] = 1
    x = d["x"].reshape(N, 8, 16, C, 4)
    x[:, :, 0] = 0
    x[:, :, 0, :, 0] = k.astype(BF)
    c = np.ones(N, np.float32)
    c[o[0]] = 0
    c[o[2]] = -1
    u = d["u"].reshape(N, 128, 128, 4)
    u[:, :, ::16] = 0
    for h in range(0, 128, 16): u[:, h, h, 0] = c.astype(BF)
    w = layers(rng)
    w[:, :, :, :, :, :8] = 0
    return {"x": x.reshape(N, 128, 4 * C), "u": u.reshape(N, 128, 512), "v": d["v"], **lists(rng), **weights(rng, w)}
def setup_inputs_near(rng):
    d = numbers_of(rng)
    o = rng.permutation(N) % 2
    k = np.where(o == 0, 2.0 ** -30, 1.0).astype(np.float32)
    x = np.zeros((N, 8, 16, C, 4), np.float32)
    s = rng.integers(-1, 2, (N, 8, C)) * k[:, None, None]
    x[:, :, 0, :, 0] = 1.125 * s
    x[:, :, 1, :, 0] = -1.25 * s
    for r in range(N):
        for g in rng.permutation(8)[:4]: x[r, g, 0, rng.integers(C), 0] = 2.0 ** 30 * rng.choice([-1.0, 1.0])
    i = np.arange(N)
    e = ((i ^ (i >> 1) ^ (i >> 2))[:, None] + rng.permutation(8)) % 2
    a = (1 + (2 * rng.integers(0, 64, (N, 8, 8, C, 4)) + 1) * 2.0 ** -7) * np.exp2(12.0 - rng.integers(8, 15, (N, 8, 8, C, 4)))
    a[:, :, 0, :, 0] = -1.96875 * 2.0 ** 12
    a = np.where(e[:, :, None, None, None] == 0, -2.0 ** 26, a)
    x[:, :, 8:] = np.where(rng.random((N, 8, 1, C, 1)) < 0.5, a, 0.0)
    u = d["u"].reshape(N, 128, 128, 4)
    u[:, :, ::16] = 0
    for h in range(0, 128, 16):
        u[:, h, h, 0] = (1.125 * k).astype(BF)
        u[:, h + 1, h, 0] = k.astype(BF)
    w = layers(rng)
    w[:, :, :8] = 0
    w[:, :, :, :, :, :8] = 0
    return {"x": x.reshape(N, 128, 4 * C).astype(BF), "u": u.reshape(N, 128, 512), "v": d["v"], **lists(rng), **weights(rng, w)}
def setup_inputs_late(rng):
    d = numbers_of(rng)
    c = (rng.permutation(N) % 2 * 2.0 - 1.0).astype(np.float32).astype(BF)
    x = d["x"].reshape(N, 8, 16, C, 4)
    x[:, :, 0] = c[:, None, None, None]
    u = d["u"].reshape(N, 128, 128, 4)
    u[:, :, ::16] = 0
    for h in range(0, 128, 16): u[:, h, h, 0] = 1
    w = layers(rng)
    w[:, :, :, :, :, 0] = (w[:, :, :, :, :, 0].astype(np.float32) * 4).astype(BF)
    return {"x": x.reshape(N, 128, 4 * C), "u": u.reshape(N, 128, 512), "v": d["v"], **lists(rng), **weights(rng, w)}
def setup_inputs_ends(rng):
    d = numbers_of(rng)
    o, e = rng.permutation(N) % 4, rng.permutation(N) % 4
    s = rng.choice([-1.0, 1.0], (N, 128, C, 4))
    s[o == 0] = -1
    s[o == 1] = rng.choice([-1.0, 1.0], (N, 1, C, 1))[o == 1]
    x = s * (0.955 + 0.02 * rng.random((N, 128, C, 4))) * 2.0 ** 30
    x[:, :8] = 0
    x[:, 13] = -240 * 2.0 ** 22
    x[:, 14] = -249 * 2.0 ** 22
    x[:, 15] = 0
    x[o == 3] = 2.0 ** -30
    size = np.where(o == 3, 2.0 ** -30, 2.0 ** 30)
    a = np.stack([rng.permutation(8) % 2 * 2.0 - 1.0 for r in range(N)]) * size[:, None]
    u = d["u"].reshape(N, 128, 128, 4)
    u[:, :, ::16] = a.astype(np.float32).astype(BF)[:, None, :, None]
    v = rng.choice([-1.0, 1.0], (N, 128, 512)) * size[:, None, None]
    t = rng.integers(0, C, (N, 8, C))
    t[o == 0] = C - 1
    t[o == 1] = 0
    t[o == 2] = rng.integers(0, 2, (8, C)) * (C - 1)
    k = rng.integers(0, C, (N, 8, 2 * C))
    k[e == 0] = C - 1
    k[e == 1] = 0
    k[e == 1, 7] = C - 1
    k[e == 2] = np.arange(2 * C) % 2 * (C - 1)
    w = np.zeros((N, 128, 4, 128, 4), np.float32)
    i = np.arange(128)
    for b in range(4):
        w[:, i, b, i, b] = np.where(o == 3, 16.0, -0.25)[:, None]
        for r in range(N):
            if o[r] < 3:
                w[r, :8, b, :8, b] = 64 * np.eye(8)
                w[r, 13:16, b, 13:16, b] = [[0, 0, -64], [0, 0, 64], [0, 0, 0]]
    return {"x": x.astype(np.float32).reshape(N, 128, 4 * C).astype(BF), "u": u.reshape(N, 128, 512), "v": v.astype(np.float32).astype(BF), **stored(k, t), **weights(rng, w.astype(BF))}
def setup_inputs_spread(rng):
    d = setup_inputs(rng)
    d["x"] = big(wide(rng, N, 128, 4 * C, cols=6))
    return d
def check_inputs(d):
    b = []
    for k in ("x", "u", "v"):
        a = np.abs(d[k].astype(np.float32))
        if not (np.isfinite(a).all() and ((a == 0) | (a >= 2.0 ** -30) & (a <= 2.0 ** 30)).all()): b.append("a value of " + k)
    for k in ("gl", "ht"):
        if not ((d[k] >= 0) & (d[k] < C)).all(): b.append("an entry of " + k)
    none, least, most = [emit(mx_ref.quantize(np.full((128, 16), k, np.float32).astype(BF)))[1][0, 0] for k in (0.0, 2.0 ** -30, 2.0 ** 30)]
    for r in range(N):
        if ((d["wc"][r] == 0x7F) | (d["wc"][r] == 0xFF)).any(): b.append("wc: a code that is no number")
        s = mx_ref.live(d["ws"][r])
        if ((s != none) & ((s < least) | (s > most))).any(): b.append("ws: a scale out of range")
        if (((d["wc"][r].reshape(16, 8, 512, 4) & 0x7F) != 0) & (s == none)[:, None, :, None]).any(): b.append("wc: a code other than zero under the scale of zeros")
    return b
def reference(x, u, v, gl, ht, wc, ws):
    qu = [mx_ref.quantize(u[r]) for r in range(N)]
    lay = [pk(wc[r], ws[r]) for r in range(N)]
    guest, host = [gentries(gl[r]) for r in range(N)], [gentries(ht[r]) for r in range(N)]
    now = [x[r] for r in range(N)]
    y, pl = np.zeros((N, 128, C), np.float32), np.zeros((N, 8, C), np.float32)
    for step in STEP:
        q = [mx_ref.quantize(now[r]) for r in range(N)]
        bit = [(mx_ref.matmul(qu[r], q[r])[::16] > 0).astype(np.int64) for r in range(N)]
        made = []
        for r in range(N):
            p = r ^ step
            at, there = np.zeros((9, C), np.int64), np.zeros((8, C), np.int64)
            at[0] = np.arange(C)
            for g in range(8):
                there[g] = host[p][g][at[g]]
                at[g + 1] = guest[r][g][2 * at[g] + bit[p][g][there[g]]]
            far = gcols(decode(q[p]).astype(BF), there)
            z = mx_ref.quantize(np.maximum(gcols(now[r], at[:8]).astype(np.float32), far.astype(np.float32)).astype(BF))
            made.append(tile([mx_ref.matmul(pick(lay[r], np.arange(128 * b, 128 * b + 128)), z) * np.float32(0.015625) + now[r][:, b::4].astype(np.float32) for b in range(4)]))
            pl[r] = at[1:]
        now = made
    oc, osc = np.zeros((N, 128, 4 * C), np.uint8), np.zeros((N, 16, C), np.uint8)
    for r in range(N):
        q = mx_ref.quantize(now[r])
        y[r] = mx_ref.matmul(mx_ref.quantize(v[r]), q)
        oc[r], osc[r] = emit(q)
    return {"y": y, "pl": pl, "oc": oc, "osc": osc}

@@ -1,0 +1,384 @@
+from concourse.bass import DstId, RemoteDMATransfer
+from concourse.mybir import dt, AluOpType, ActivationFunctionType
+
+C = 352
+STEP = [1, 2, 4]
+L = C // 16
+LA = 12
+PARTS = [(0, 16 * LA), (16 * LA, C)]
+SLOTS = 8
+F8 = "float8_e4m3fn_x4"
+
+SCRATCH = {
+    "ut": ("sbuf", [128, 512], "bfloat16"), "uq": ("sbuf", [128, 128], F8), "us": ("sbuf", [128, 128], "uint8"),
+    "uqp": ("sbuf", [128, 256], F8), "usp": ("sbuf", [128, 256], "uint8"),
+    "vt": ("sbuf", [128, 512], "bfloat16"), "vq": ("sbuf", [128, 128], F8), "vs": ("sbuf", [128, 128], "uint8"),
+    "wq": ("sbuf", [128, 512], F8), "wsc": ("sbuf", [128, 512], "uint8"),
+    "idn1": ("sbuf", [128, 128], "float32"), "idn": ("sbuf", [128, 128], "float32"),
+    "et": ("sbuf", [128, 2048], "bfloat16"), "eq": ("sbuf", [128, 512], F8), "es": ("sbuf", [128, 512], "uint8"),
+    "hti": ("sbuf", [128, 2 * L], "int32"), "htj": ("sbuf", [128, L], "int32"),
+    "hto": ("sbuf", [128, 2 * L], "uint16"), "htn": ("sbuf", [128, L], "uint16"),
+    "glc": ("dram", [8, 2 * 88 * SLOTS], "int32"), "eo": ("sbuf", [128, 88 * SLOTS], "int32"),
+    "pc": ("sbuf", [128, 1], "int32"), "pi": ("sbuf", [128, 8], "int32"),
+    "pf": ("sbuf", [128, 4], "float32"), "bc": ("sbuf", [128, 1], "float32"), "ini": ("sbuf", [128, 1], "float32"),
+    "uoi": ("sbuf", [128, 16], "int32"), "uoj": ("sbuf", [128, 16], "int32"), "uou": ("sbuf", [128, 16], "uint16"),
+    "jm": ("sbuf", [128, C], "float32"), "ramp": ("sbuf", [128, C], "float32"), "jv": ("sbuf", [128, L * SLOTS], "float32"),
+    "jp": ("sbuf", [128, L * SLOTS], "float32"), "hlf": ("sbuf", [128, L * SLOTS], "float32"), "mh": ("sbuf", [128, L * SLOTS], "float32"),
+    "mc": ("sbuf", [128, L * SLOTS], "float32"), "ji": ("sbuf", [128, L * SLOTS], "float32"),
+    "mask": ("sbuf", [128, C], "bfloat16"), "keep": ("sbuf", [128, C], "bfloat16"),
+    "mask2": ("sbuf", [128, C], "float32"), "a0": ("sbuf", [128, C], "float32"),
+    "t1": ("sbuf", [128, 44 * SLOTS], "float32"), "t2": ("sbuf", [128, 44 * SLOTS], "float32"), "sel": ("sbuf", [128, 44 * SLOTS], "float32"),
+    "sm": ("sbuf", [128, L * SLOTS], "float32"), "df": ("sbuf", [128, L * SLOTS], "float32"),
+    "em": ("sbuf", [128, L * SLOTS], "float32"), "etab": ("sbuf", [128, L * SLOTS], "float32"), "dtab": ("sbuf", [128, L * SLOTS], "float32"),
+    "zb": ("sbuf", [128, 2 * L], "bfloat16"),
+    "sg": ("sbuf", [128, 2 * C], "bfloat16"), "gm": ("sbuf", [128, 2 * C], "bfloat16"), "sc": ("sbuf", [128, 2 * C], "bfloat16"),
+    "nt": ("sbuf", [128, L * SLOTS], "float32"), "nf": ("sbuf", [128, L * SLOTS], "float32"), "nu": ("sbuf", [128, L * SLOTS], "uint16"),
+    "ya": ("sbuf", [128, C], "float32"), "yb": ("sbuf", [128, C], "float32"), "plr": ("sbuf", [128, C], "float32"),
+    "mk2": ("sbuf", [128, C], "float32"), "sc2": ("sbuf", [128, C], "float32"), "vl": ("sbuf", [128, L], "uint16"),
+    "x64": ("sbuf", [128, 4 * C], "bfloat16"), "ds": ("sbuf", [128, 4 * C], "bfloat16"), "mm": ("sbuf", [128, 4 * C], "bfloat16"),
+    "tf": ("sbuf", [128, 4 * C], "float32"), "yt": ("sbuf", [128, C], "float32"),
+    "pd": ("psum", [128, 2048], "float32"), "pw": ("psum", [128, 2048], "float32"),
+    "hr": ("sbuf", [128, L], "uint16"), "lb": ("dram", [640, 2 * L], "bfloat16"),
+}
+for _k in range(4):
+    SCRATCH["xt%d" % _k] = ("sbuf", [128, 4 * C], "bfloat16")
+    SCRATCH["xq%d" % _k] = ("sbuf", [128, C], F8)
+    SCRATCH["xs%d" % _k] = ("sbuf", [128, C], "uint8")
+for _k in range(3):
+    SCRATCH["rc%d" % _k] = ("sbuf", [128, C], F8)
+    SCRATCH["rs%d" % _k] = ("sbuf", [128, C], "uint8")
+    SCRATCH["zt%d" % _k] = ("sbuf", [128, 4 * C], "bfloat16")
+    SCRATCH["zq%d" % _k] = ("sbuf", [128, C], F8)
+    SCRATCH["zs%d" % _k] = ("sbuf", [128, C], "uint8")
+    SCRATCH["bl%d" % _k] = ("sbuf", [128, 2 * L], "bfloat16")
+    SCRATCH["bb%d" % _k] = ("sbuf", [128, L * SLOTS], "bfloat16")
+    SCRATCH["hq%d" % _k] = ("sbuf", [128, L], "uint16")
+    SCRATCH["ca%d" % _k] = ("sbuf", [128, 16 * LA], F8)
+    SCRATCH["sa%d" % _k] = ("sbuf", [128, C], "uint8")
+
+SEMAPHORES = ["ve", "se", "pe", "gp", "dx", "du", "dn", "dh", "dg", "dw", "dv", "de", "do", "sent", "rz", "rh"]
+for _k in range(3):
+    SEMAPHORES += ["c%d" % _k, "ba%d" % _k, "bz%d" % _k, "h%d" % _k, "rc%d" % _k, "rb%d" % _k]
+
+
+def share(topo, src, dst, i, n):
+    return topo.engines(src, dst)[i::n]
+
+
+def send(g, core, T, topo, parts, n):
+    ts, total = [], 0
+    for i, (dst, a, b, sem) in enumerate(parts):
+        e = share(topo, core, dst, i, n)
+        rid, pid = topo.addr(dst, core)
+        ts.append(RemoteDMATransfer(dst_ids=[DstId(rid=rid, pnc=pid)], dma_engine_mask=sum(1 << j for j in e), remote_sem=T.sem[sem], srcs=[a], dsts=[b]))
+        total += len(e)
+    g.remote_dma_fused(ts, local_sem=T.sem.sent)
+    return total
+
+
+def handers(topo, core, partner):
+    r = [c for c in topo.cores_of(core) if c != core and topo.may_write(c, partner)]
+    return [c for c in r if topo.die(c) == topo.die(core)], [c for c in r if topo.die(c) != topo.die(core)]
+
+
+def host_tables(near, far):
+    return [(near[0], 0, 0, L), (far[0], 1, 0, L), (near[1], 2, 0, LA), (far[1], 2, LA, L)]
+
+
+def u8(v):
+    return v.bitcast(dt.uint8)
+
+
+def hand_on(g, core, T, topo, home, near, far):
+    rank = T.rank_of(home)
+    mates = [T.cores[rank ^ s] for s in STEP]
+    sent = 0
+    for i, (c, k, a, e) in enumerate(host_tables(near, far)):
+        if c == core:
+            g.wait_ge(T.sem.rh, len(share(topo, home, core, i, 4)))
+            sent += send(g, core, T, topo, [(mates[k], T.hr[:, a:e], T["hq%d" % k][:, a:e], "h%d" % k)], 1)
+    if core in (near[0], far[0]):
+        a, e = PARTS[0 if core == near[0] else 1]
+        for k in range(3):
+            g.wait_ge(T.sem["rc%d" % k], len(share(topo, home, core, 0, 1)))
+            sent += send(g, core, T, topo, [(mates[k], u8(T["ca%d" % k][:, 0:e - a]), u8(T["rc%d" % k][:, a:e]), "c%d" % k)], 1)
+    else:
+        i = 0 if core == near[1] else 1
+        g.wait_ge(T.sem.rz, len(share(topo, home, core, i, 2)))
+        for k in range(3):
+            if not i:
+                g.wait_ge(T.sem["rc%d" % k], len(share(topo, home, core, 0, 1)))
+                sent += send(g, core, T, topo, [(mates[k], T["sa%d" % k][:, :], T["rs%d" % k][:, :], "c%d" % k)], 1)
+            if k < 2:
+                g.wait_ge(T.sem["rb%d" % k], len(share(topo, home, core, i, 2)))
+                base = 128 * (k + 1)
+            else:
+                g.wait_ge(T.sem["rb%d" % k], 2 * len(share(topo, home, core, 0, 4)))
+                base = 512
+            parts = []
+            for m in (2 * i, 2 * i + 1):
+                a = base - 32 * m
+                parts.append((mates[k], T.lb[a:a + 128, :], T["bb%d" % k][:, 2 * L * m:2 * L * (m + 1)], ("bz%d" if i else "ba%d") % k))
+            sent += send(g, core, T, topo, parts, 2)
+    g.wait_ge(T.sem.sent, sent)
+
+
+def rank_program(g, core, T, topo):
+    rank = T.rank_of(core)
+    if rank is None:
+        for home in T.cores:
+            if core in topo.cores_of(home):
+                near, far = handers(topo, home, T.cores[T.rank_of(home) ^ STEP[0]])
+                if core in near[:2] + far[:2]:
+                    hand_on(g, core, T, topo, home, near, far)
+        return
+    A, AF = AluOpType, ActivationFunctionType
+    mates = [T.cores[rank ^ s] for s in STEP]
+    near, far = handers(topo, core, mates[0])
+    queue = {"ve": g.vector, "se": g.scalar, "pe": g.tensor, "gp": g, "sy": g.sync}
+    count, seen, sent = {"ve": 0, "se": 0, "pe": 0, "gp": 0}, {}, [0]
+
+    def need(e, *toks):
+        for t in toks:
+            if isinstance(t, list):
+                need(e, *t)
+            elif t is not None and seen.get((e, t[0]), 0) < t[1]:
+                queue[e].wait_ge(T.sem[t[0]], t[1])
+                seen[(e, t[0])] = t[1]
+
+    def op(e, call, *deps):
+        need(e, *deps)
+        count[e] += 1
+        call().then_inc(T.sem[e], 1)
+        return (e, count[e])
+
+    v, s, p = g.vector, g.scalar, g.tensor
+
+    def ts(out, in0, s1, s2, o0, o1=None, deps=()):
+        if o1 is None:
+            return op("ve", lambda: v.tensor_scalar(out, in0, s1, None, o0), *deps)
+        return op("ve", lambda: v.tensor_scalar(out, in0, s1, s2, o0, o1), *deps)
+
+    def tt(out, a, b, o, *deps):
+        return op("ve", lambda: v.tensor_tensor(out, a, b, o), *deps)
+
+    def cp(out, a, *deps):
+        return op("ve", lambda: v.tensor_copy(out, a), *deps)
+
+    def ms(ap, c, *deps):
+        return op("ve", lambda: v.memset(ap, c), *deps)
+
+    def qu(q, qs, t, *deps):
+        return op("ve", lambda: v.quantize_mx(q, qs, t), *deps)
+
+    def act(out, a, *deps, scale=1.0):
+        if scale == 1.0:
+            return op("se", lambda: s.activation(out, a, AF.Copy), *deps)
+        return op("se", lambda: s.activation(out, a, AF.Copy, scale=scale), *deps)
+
+    def mm(out, q, qs, x, xs, *deps):
+        return op("pe", lambda: p.matmul_mx(out, q, qs, x, xs, True, True), *deps)
+
+    def out_to(parts, n):
+        sent[0] += send(g, core, T, topo, parts, n)
+
+    g.sync.dma_start(T.htj[:, :], T.ht[:, :]).then_inc(T.sem.dn, 16)
+    g.sync.dma_start(T.ut[:, :], T.u[:, :]).then_inc(T.sem.du, 16)
+    g.sync.dma_start(T.xt0[:, :], T.x[:, :]).then_inc(T.sem.dx, 16)
+    for d in range(2):
+        w = 16 * (d + 1)
+        g.sync.dma_start(T.hti[w:128, L * d:L * d + L], T.ht[0:128 - w, :]).then_inc(T.sem.dh, 16)
+        g.sync.dma_start(T.hti[0:w, L * d:L * d + L], T.ht[128 - w:128, :]).then_inc(T.sem.dh, 16)
+    for i in range(16):
+        a = i % 8
+        g.scalar.dma_start(T.glc[:, 88 * i:88 * i + 88], T.gl[16 * a:16 * a + 16, :]).then_inc(T.sem.dg, 16)
+    need("sy", ("dg", 256))
+    for i in range(16):
+        a = i // 2
+        g.sync.dma_start(T.eo[8 * i:8 * i + 8, :], T.glc[:, 88 * a:88 * a + 88 * SLOTS]).then_inc(T.sem.de, 16)
+
+    def iota(ap, pat, base, cm, f=False):
+        if f:
+            return op("gp", lambda: g.iota(ap, pat, base, cm, allow_small_or_imprecise_dtypes=True))
+        return op("gp", lambda: g.iota(ap, pat, base, cm))
+    k_zb = ms(T.zb[:, :], 0.0)
+    k_et = ms(T.et[:, :], 0.0)
+    k_one = ms(T.idn1[:, :], 1.0)
+    k_hlf = ms(T.hlf[:, :], 0.5)
+    k_bc = ms(T.bc[:, :], -2.0 ** -110)
+    g_pc = iota(T.pc[:, :], [[1, 1]], 0, 1)
+    g_uo = iota(T.uoi[:, :], [[-16, 2], [16, 8]], 112, 0)
+    g_jm = iota(T.jm[:, :], [[0, L], [1, 16]], 0, 0, True)
+    need("gp", k_zb)
+    out_to([(near[1], T.zb[:, :], T.lb[0:128, :], "rz"), (far[1], T.zb[:, :], T.lb[0:128, :], "rz")], 2)
+    k_p15 = ts(T.pi[:, 0:1], T.pc[:, :], 15, None, A.bitwise_and, deps=(g_pc,))
+    k_h = ts(T.pi[:, 1:2], T.pc[:, :], 3, 1, A.logical_shift_right, A.bitwise_and)
+    k_uo = ts(T.uoj[:, :], T.uoi[:, :], 127, None, A.bitwise_and, deps=(g_uo,))
+    k_pf = cp(T.pf[:, 0:2], T.pi[:, 0:2], k_p15, k_h)
+    k_uu = cp(T.uou[:, :], T.uoj[:, :], k_uo)
+    k_nh = ts(T.pf[:, 2:3], T.pf[:, 1:2], -1.0, 1.0, A.mult, A.add, deps=(k_pf,))
+    k_mask = ts(T.mask[:, :], T.jm[:, :], T.pf[:, 0:1], None, A.is_equal, deps=(g_jm, k_pf))
+    k_keep = ts(T.keep[:, :], T.jm[:, :], T.pf[:, 0:1], None, A.not_equal)
+    k_htn = cp(T.htn[:, :], T.htj[:, :], ("dn", 16))
+    m2 = cp(T.mask2[:, :], T.mask[:, :], k_mask)
+    m2 = ms(T.mask2[0:16, :], 0.0, m2)
+    k_u = qu(T.uq[:, :], T.us[:, :], T.ut[:, :], ("du", 16))
+    k_up = cp(T.uqp[:, :].bitcast(dt.uint32), T.uq[:, :].bitcast(dt.uint32).indirect(T.uou[:, :]), k_u, k_uu)
+    k_us = act(T.usp[:, :], T.us[:, :].indirect(T.uou[:, :]), k_u, k_uu)
+    need("gp", k_htn)
+    out_to([(c, T.htn[:, :], T.hr[:, :], "rh") for c, _, _, _ in host_tables(near, far)], 4)
+
+    xtok, pdread, addread = [[("dx", 16)], [("dx", 16)]], [], []
+    for k in range(4):
+        xt, xq, xs = T["xt%d" % k], T["xq%d" % k], T["xs%d" % k]
+        q0 = []
+        for i, (a, e) in enumerate(PARTS):
+            q0.append(qu(xq[:, a:e], xs[:, a:e], xt[:, 4 * a:4 * e], xtok[i]))
+            if k < 3:
+                need("gp", q0[i])
+                out_to([((near[0], far[0])[i], u8(xq[:, a:e]), u8(T["ca%d" % k][:, 0:e - a]), "rc%d" % k)], 1)
+        if k == 3:
+            break
+        rc, rs, bl, bb, hq = T["rc%d" % k], T["rs%d" % k], T["bl%d" % k], T["bb%d" % k], T["hq%d" % k]
+        zt, zq, zs, xn = T["zt%d" % k], T["zq%d" % k], T["zs%d" % k], T["xt%d" % (k + 1)]
+        back = handers(topo, mates[k], core)
+        out_to([(near[1], xs[:, :], T["sa%d" % k][:, :], "rc%d" % k)], 1)
+        if k == 0:
+            g_id = op("gp", lambda: g.affine_select(T.idn[:, :], T.idn1[:, :], [[-1, 128]], A.is_equal, 0.0, 0, 1), k_one)
+            k_hto = cp(T.hto[:, :], T.hti[:, :], ("dh", 64))
+        sgn = []
+        for d in range(2):
+            m = mm(T.pd[:, 512 * d:512 * d + C], T.uqp[:, 128 * d:128 * d + 128], T.usp[:, 128 * d:128 * d + 128], xq[:, :], xs[:, :], q0, k_up, k_us, pdread)
+            need("se", m, k_bc)
+            sgn.append(op("se", lambda d=d: s.activation(T.sg[:, C * d:C * d + C], T.pd[:, 512 * d:512 * d + C], AF.Sign, bias=T.bc[:, 0:1])))
+        k64 = act(T.x64[:, :], xt[:, :], xtok, scale=64.0)
+        gs = [tt(T.gm[:, C * d:C * d + C], T.sg[:, C * d:C * d + C].indirect(T.hto[:, L * d:L * d + L]), T.mask[:, :], A.mult, sgn[d], k_hto, k_mask) for d in range(2)]
+        sc = [op("ve", lambda d=d: v.tensor_tensor_scan(T.sc[:, C * d:C * d + C], T.keep[:, :], T.gm[:, C * d:C * d + C], 0.0, A.mult, A.add), gs[d], k_keep) for d in range(2)]
+        k_bl = cp(bl[:, :], T.sc[:, 15:2 * C:16], sc)
+        need("gp", k_bl)
+        if k < 2:
+            a = 128 * (k + 1)
+            out_to([(c, bl[:, :], T.lb[a:a + 128, :], "rb%d" % k) for c in (near[1], far[1])], 2)
+        else:
+            out_to([(c, bl[:, :], T.lb[a:a + 128, :], "rb%d" % k) for a in (384, 512) for c in (near[1], far[1])], 4)
+        if k == 0:
+            g_jv = iota(T.jv[:, :], [[0, SLOTS], [16, L]], 0, 0, True)
+            g_mh = op("gp", lambda: g.affine_select(T.mh[:, :], T.hlf[:, :], [[-16, SLOTS], [0, L]], A.is_ge, 0.0, -16, 1), k_hlf)
+            g_rm = iota(T.ramp[:, :], [[1, C]], 0, 0, True)
+            ec = [cp(T.et[:, 512 * b + b:512 * b + 512:4], T.idn[:, :], k_et, g_id) for b in range(4)]
+            a0 = ts(T.a0[:, :], T.mask[:, :], -1000.0, None, A.mult)
+            a0 = ts(T.a0[0:16, :], T.jm[0:16, :], 0.0, 16.0, A.is_equal, A.mult, deps=(a0,))
+            a0 = ms(T.a0[0:16, 0:1], 0.0, a0)
+            i0 = ms(T.ini[:, :], 0.0)
+            k_eq = qu(T.eq[:, :], T.es[:, :], T.et[:, :], ec)
+            i0 = cp(T.ini[0:16, :], T.pf[0:16, 0:1], i0)
+            k_static = [m2, a0, i0]
+            mh = ms(T.mh[0:16, :], 0.5, g_mh)
+            jp = ts(T.jp[:, :], T.jv[:, :], T.pf[:, 0:1], None, A.add, deps=(g_jv,))
+            mc = ts(T.mc[:, :], T.mh[:, :], -2.0, 1.0, A.mult, A.add, deps=(mh,))
+            ji = tt(T.ji[:, :], T.jp[:, :], T.mc[:, :], A.mult, jp, mc)
+            e1 = ts(T.t1[:, :], T.eo[:, 0:88 * SLOTS:2], T.pf[:, 2:3], None, A.mult, deps=(("de", 256), k_nh))
+            e2 = ts(T.t2[:, :], T.eo[:, 1:88 * SLOTS:2], T.pf[:, 1:2], None, A.mult)
+            e3 = tt(T.sel[:, :], T.t1[:, :], T.t2[:, :], A.add, e1, e2)
+            for d in range(SLOTS):
+                c = 44 * (SLOTS - 1 - d)
+                ee, oo = T.sel[:, c:c + L], T.sel[:, c + L:c + 2 * L]
+                sm = tt(T.sm[:, L * d:L * d + L], ee, oo, A.add, e3)
+                df = tt(T.df[:, L * d:L * d + L], oo, ee, A.subtract)
+            em = tt(T.em[:, :], T.sm[:, :], T.mh[:, :], A.mult, sm)
+            dtb = tt(T.dtab[:, :], T.df[:, :], T.mh[:, :], A.mult, df)
+            etb = tt(T.etab[:, :], T.em[:, :], T.ji[:, :], A.add, em, ji)
+            k_tab = [dtb, etb]
+        call = ("c%d" % k, sum(len(share(topo, c, core, 0, 1)) for c in (back[0][0], back[1][0], back[0][1])))
+        if k == 0:
+            need("sy", call)
+            g.sync.dma_start(u8(T.wq[:, :]), T.wc[:, :]).then_inc(T.sem.dw, 16)
+            g.sync.dma_start(T.wsc[:, :], T.ws[:, :]).then_inc(T.sem.dw, 16)
+            g.sync.dma_start(T.vt[:, :], T.v[:, :]).then_inc(T.sem.dv, 16)
+        dc = []
+        for b in range(4):
+            m = mm(T.pd[:, 512 * b:512 * b + C], T.eq[:, 128 * b:128 * b + 128], T.es[:, 128 * b:128 * b + 128], rc[:, :], rs[:, :], call, k_eq, sgn)
+            dc.append(act(T.ds[:, C * b:C * b + C], T.pd[:, 512 * b:512 * b + C], m))
+        pdread = dc
+        hs = ("h%d" % k, sum(len(share(topo, c, core, 0, 1)) for c, kk, _, _ in host_tables(*back) if kk == k))
+
+        def larger(b):
+            return tt(T.mm[:, C * b:C * b + C], T.ds[:, C * b:C * b + C].indirect(hq[:, :]), xt[:, b:4 * C:4], A.max, dc[b], hs)
+
+        def lists(a, e, *deps):
+            n1 = tt(T.nt[:, a:e], bb[:, a:e], T.dtab[:, a:e], A.mult, k_tab, *deps)
+            n2 = tt(T.nf[:, a:e], T.nt[:, a:e], T.etab[:, a:e], A.add, n1)
+            return cp(T.nu[:, a:e], T.nf[:, a:e], n2)
+        ba = ("ba%d" % k, 2 * len(share(topo, back[0][1], core, 0, 2)))
+        bz = ("bz%d" % k, 2 * len(share(topo, back[1][1], core, 0, 2)))
+        lg = [larger(b) for b in range(3)]
+        n1 = lists(0, 2 * L, ba)
+        n2 = lists(2 * L, L * SLOTS, bz)
+        lg += [larger(3)]
+        win, tok, ys = T.ramp, [g_rm], [T.ya, T.yb]
+        for d in range(6):
+            o, n = ys[d % 2], n1 if d < 2 else n2
+            c = L * d
+            if d < 2:
+                tok = [act(o[:, :], win[:, :].indirect(T.nu[:, c:c + L]), tok, n)]
+            else:
+                h = 16 * LA
+                tok = [cp(o[:, 0:h], win[:, :].indirect(T.nu[:, c:c + LA]), tok, n), act(o[:, h:C], win[:, :].indirect(T.nu[:, c + LA:c + L]), tok, n)]
+            win = o
+        c6 = tt(T.mk2[:, :], win[:, :].indirect(T.nu[:, 6 * L:7 * L]), T.mask2[:, :], A.mult, tok, k_static)
+        c7 = op("ve", lambda: v.tensor_tensor_scan(T.sc2[:, :], T.a0[:, :], T.mk2[:, :], T.ini[:, 0:1], A.add, A.max), c6)
+        k_vl = cp(T.vl[:, :], T.sc2[:, 15:C:16], c7)
+        zc = [[], []]
+
+        def mosaic(i, b, e):
+            a, z = PARTS[i]
+            o, w = zt[:, 4 * a + b:4 * z:4], T.mm[:, C * b:C * b + C].indirect(T.vl[:, a // 16:z // 16])
+            zc[i].append(cp(o, w, k_vl, lg) if e == "ve" else act(o, w, k_vl, lg))
+        for i, b, e in ((0, 0, "ve"), (0, 2, "se"), (0, 1, "ve"), (0, 3, "se"), (1, 0, "ve"), (1, 2, "se"), (1, 3, "se"), (1, 1, "se")):
+            mosaic(i, b, e)
+        if k == 2:
+            o = ys[0]
+            t6 = act(o[:, :], win[:, :].indirect(T.nu[:, 6 * L:7 * L]), tok)
+        xtok = [[], []]
+
+        def layer(i):
+            a, z = PARTS[i]
+            qz = qu(zq[:, a:z], zs[:, a:z], zt[:, 4 * a:4 * z], zc[i])
+            ps = (T.pw, T.pd)[i]
+            return [mm(ps[:, 512 * b:512 * b + z - a], T.wq[:, 128 * b:128 * b + 128], T.wsc[:, 128 * b:128 * b + 128], zq[:, a:z], zs[:, a:z], qz, ("dw", 32), pdread, addread) for b in range(4)]
+
+        def state(i, b, m):
+            a, z = PARTS[i]
+            ps = (T.pw, T.pd)[i]
+            ad = tt(T.tf[:, C * b + a:C * b + z], ps[:, 512 * b:512 * b + z - a], T.x64[:, 4 * a + b:4 * z:4], A.add, m, k64)
+            xtok[i].append(act(xn[:, 4 * a + b:4 * z:4], T.tf[:, C * b + a:C * b + z], ad, scale=2.0 ** -6))
+            return ad
+        ma = layer(0)
+        mb = layer(1)
+        addread = [state(0, b, ma[b]) for b in range(4)] + [state(1, b, mb[b]) for b in range(4)]
+        pdread = pdread + addread
+        if k == 0:
+            k_v = qu(T.vq[:, :], T.vs[:, :], T.vt[:, :], ("dv", 16))
+        if k == 2:
+            pltok = act(T.plr[:, :], ys[0][:, :].indirect(T.nu[:, 7 * L:8 * L]), t6)
+
+    do = [0]
+
+    def store(out, a, *deps):
+        need("sy", *deps)
+        g.sync.dma_start(out, a).then_inc(T.sem.do, 16)
+        do[0] += 16
+    yc = []
+    for i, (a, e) in enumerate(PARTS):
+        m = mm(T.pd[:, 512 * i:512 * i + e - a], T.vq[:, :], T.vs[:, :], T.xq3[:, a:e], T.xs3[:, a:e], q0[i], k_v, pdread)
+        yc.append(cp(T.yt[:, a:e], T.pd[:, 512 * i:512 * i + e - a], m) if i else act(T.yt[:, a:e], T.pd[:, 0:e - a], m))
+    store(T.oc[:, :], u8(T.xq3[:, :]), q0)
+    for b in range(4):
+        store(T.osc[4 * b:4 * b + 4, :], T.xs3[32 * b:32 * b + 4, :])
+    store(T.y[:, :], T.yt[:, :], yc)
+    store(T.pl[0:7, :], T.plr[16:128:16, :], pltok)
+    store(T.pl[7:8, :], T.plr[0:1, :])
+    g.sync.wait_ge(T.sem.do, do[0])
+    for e in ("ve", "se", "pe", "gp"):
+        need("gp", (e, count[e]))
+    g.wait_ge(T.sem.sent, sent[0])

@@ -6,8 +6,9 @@ STEP = [1, 2, 4]
 L = C // 16
 LA = 12
 PARTS = [(0, 16 * LA), (16 * LA, C)]
-SLOTS = 8
 F8 = "float8_e4m3fn_x4"
+K = 512.0
+BANK = 512
 
 SCRATCH = {
     "ut": ("sbuf", [128, 512], "bfloat16"), "uq": ("sbuf", [128, 128], F8), "us": ("sbuf", [128, 128], "uint8"),
@@ -18,27 +19,28 @@ SCRATCH = {
     "et": ("sbuf", [128, 2048], "bfloat16"), "eq": ("sbuf", [128, 512], F8), "es": ("sbuf", [128, 512], "uint8"),
     "hti": ("sbuf", [128, 2 * L], "int32"), "htj": ("sbuf", [128, L], "int32"),
     "hto": ("sbuf", [128, 2 * L], "uint16"), "htn": ("sbuf", [128, L], "uint16"),
-    "glc": ("dram", [8, 2 * 88 * SLOTS], "int32"), "eo": ("sbuf", [128, 88 * SLOTS], "int32"),
-    "pc": ("sbuf", [128, 1], "int32"), "pi": ("sbuf", [128, 8], "int32"),
-    "pf": ("sbuf", [128, 4], "float32"), "bc": ("sbuf", [128, 1], "float32"), "ini": ("sbuf", [128, 1], "float32"),
+    "gd": ("dram", [10, 64 * L], "int32"), "eo": ("sbuf", [128, 8 * L], "int32"),
+    "pc": ("sbuf", [128, 1], "int32"), "pi": ("sbuf", [128, 8], "int32"), "pf": ("sbuf", [128, 8], "float32"),
+    "bc": ("sbuf", [128, 1], "float32"), "cw": ("sbuf", [128, 2], "float32"), "cv": ("sbuf", [128, 1], "float32"),
+    "iv": ("sbuf", [128, 1], "float32"), "xb0": ("sbuf", [128, 4 * C], "bfloat16"), "xb1": ("sbuf", [128, 4 * C], "bfloat16"),
     "uoi": ("sbuf", [128, 16], "int32"), "uoj": ("sbuf", [128, 16], "int32"), "uou": ("sbuf", [128, 16], "uint16"),
-    "jm": ("sbuf", [128, C], "float32"), "ramp": ("sbuf", [128, C], "float32"), "jv": ("sbuf", [128, L * SLOTS], "float32"),
-    "jp": ("sbuf", [128, L * SLOTS], "float32"), "hlf": ("sbuf", [128, L * SLOTS], "float32"), "mh": ("sbuf", [128, L * SLOTS], "float32"),
-    "mc": ("sbuf", [128, L * SLOTS], "float32"), "ji": ("sbuf", [128, L * SLOTS], "float32"),
-    "mask": ("sbuf", [128, C], "bfloat16"), "keep": ("sbuf", [128, C], "bfloat16"),
-    "mask2": ("sbuf", [128, C], "float32"), "a0": ("sbuf", [128, C], "float32"),
-    "t1": ("sbuf", [128, 44 * SLOTS], "float32"), "t2": ("sbuf", [128, 44 * SLOTS], "float32"), "sel": ("sbuf", [128, 44 * SLOTS], "float32"),
-    "sm": ("sbuf", [128, L * SLOTS], "float32"), "df": ("sbuf", [128, L * SLOTS], "float32"),
-    "em": ("sbuf", [128, L * SLOTS], "float32"), "etab": ("sbuf", [128, L * SLOTS], "float32"), "dtab": ("sbuf", [128, L * SLOTS], "float32"),
-    "zb": ("sbuf", [128, 2 * L], "bfloat16"),
-    "sg": ("sbuf", [128, 2 * C], "bfloat16"), "gm": ("sbuf", [128, 2 * C], "bfloat16"), "sc": ("sbuf", [128, 2 * C], "bfloat16"),
-    "nt": ("sbuf", [128, L * SLOTS], "float32"), "nf": ("sbuf", [128, L * SLOTS], "float32"), "nu": ("sbuf", [128, L * SLOTS], "uint16"),
+    "ji": ("sbuf", [128, 16], "int32"), "jr": ("sbuf", [128, 16], "int32"),
+    "f1": ("sbuf", [128, 32], "float32"), "f3": ("sbuf", [128, 16], "float32"), "f4": ("sbuf", [128, 16], "float32"),
+    "ramp": ("sbuf", [128, C], "float32"), "jv": ("sbuf", [128, 2 * L], "float32"), "jp": ("sbuf", [128, 2 * L], "float32"),
+    "jm": ("sbuf", [128, 2 * L], "float32"), "per": ("sbuf", [128, L], "uint16"),
+    "fw": ("sbuf", [128, C], "bfloat16"), "fv": ("sbuf", [128, C], "bfloat16"),
+    "t1": ("sbuf", [128, 4 * L], "float32"), "t2": ("sbuf", [128, 4 * L], "float32"), "sel": ("sbuf", [128, 4 * L], "float32"),
+    "selb": ("sbuf", [128, 2 * L], "float32"), "selc": ("sbuf", [128, 2 * L], "float32"),
+    "gt0": ("sbuf", [128, 4 * L], "uint16"), "gf": ("sbuf", [128, 4 * L], "float32"), "kd": ("sbuf", [128, 2 * L], "float32"),
+    "sg": ("sbuf", [128, 2 * C], "bfloat16"), "gm": ("sbuf", [128, 2 * C], "bfloat16"), "sc": ("sbuf", [128, 2 * C], "float16"),
+    "bl": ("sbuf", [128, 2 * L], "float32"), "bb": ("sbuf", [128, 2 * L], "float32"),
+    "nt": ("sbuf", [128, 2 * L], "float32"), "nf": ("sbuf", [128, 2 * L], "float32"), "nu": ("sbuf", [128, 2 * L], "uint16"),
     "ya": ("sbuf", [128, C], "float32"), "yb": ("sbuf", [128, C], "float32"), "plr": ("sbuf", [128, C], "float32"),
-    "mk2": ("sbuf", [128, C], "float32"), "sc2": ("sbuf", [128, C], "float32"), "vl": ("sbuf", [128, L], "uint16"),
-    "x64": ("sbuf", [128, 4 * C], "bfloat16"), "ds": ("sbuf", [128, 4 * C], "bfloat16"), "mm": ("sbuf", [128, 4 * C], "bfloat16"),
-    "tf": ("sbuf", [128, 4 * C], "float32"), "yt": ("sbuf", [128, C], "float32"),
-    "pd": ("psum", [128, 2048], "float32"), "pw": ("psum", [128, 2048], "float32"),
-    "hr": ("sbuf", [128, L], "uint16"), "lb": ("dram", [640, 2 * L], "bfloat16"),
+    "sp": ("sbuf", [128, C], "float32"), "sv": ("sbuf", [128, C], "float32"), "slot": ("sbuf", [128, 4 * L], "uint16"),
+    "l2": ("sbuf", [128, L], "uint16"), "rp": ("sbuf", [128, L], "uint16"),
+    "ds": ("sbuf", [128, 4 * C], "bfloat16"), "mm": ("sbuf", [128, 4 * C], "bfloat16"), "yt": ("sbuf", [128, C], "float32"),
+    "ps": ("psum", [128, 8 * BANK], "float32"),
+    "hr": ("sbuf", [128, L], "uint16"), "gr": ("sbuf", [128, 4 * L], "uint16"), "br": ("sbuf", [128, 2 * L], "float32"), "pr": ("sbuf", [128, L], "uint16"),
 }
 for _k in range(4):
     SCRATCH["xt%d" % _k] = ("sbuf", [128, 4 * C], "bfloat16")
@@ -50,15 +52,20 @@ for _k in range(3):
     SCRATCH["zt%d" % _k] = ("sbuf", [128, 4 * C], "bfloat16")
     SCRATCH["zq%d" % _k] = ("sbuf", [128, C], F8)
     SCRATCH["zs%d" % _k] = ("sbuf", [128, C], "uint8")
-    SCRATCH["bl%d" % _k] = ("sbuf", [128, 2 * L], "bfloat16")
-    SCRATCH["bb%d" % _k] = ("sbuf", [128, L * SLOTS], "bfloat16")
     SCRATCH["hq%d" % _k] = ("sbuf", [128, L], "uint16")
+    SCRATCH["vl%d" % _k] = ("sbuf", [128, L], "uint16")
+    SCRATCH["dtab%d" % _k] = ("sbuf", [128, 2 * L], "float32")
+    SCRATCH["etab%d" % _k] = ("sbuf", [128, 2 * L], "float32")
     SCRATCH["ca%d" % _k] = ("sbuf", [128, 16 * LA], F8)
     SCRATCH["sa%d" % _k] = ("sbuf", [128, C], "uint8")
+for _k in (1, 2):
+    SCRATCH["gt%d" % _k] = ("sbuf", [128, 4 * L], "uint16")
+    SCRATCH["vr%d" % _k] = ("sbuf", [128, L], "uint16")
+    SCRATCH["rv%d" % _k] = ("sbuf", [128, L], "uint16")
 
-SEMAPHORES = ["ve", "se", "pe", "gp", "dx", "du", "dn", "dh", "dg", "dw", "dv", "de", "do", "sent", "rz", "rh"]
+SEMAPHORES = ["ve", "se", "pe", "gp", "dx0", "dx1", "du", "dn", "dh", "dg", "dw", "dv", "de", "do", "sent", "rh", "rg", "rl", "pl"]
 for _k in range(3):
-    SEMAPHORES += ["c%d" % _k, "ba%d" % _k, "bz%d" % _k, "h%d" % _k, "rc%d" % _k, "rb%d" % _k]
+    SEMAPHORES += ["c%d" % _k, "m%d" % _k, "h%d" % _k, "g%d" % _k, "rc%d" % _k, "rm%d" % _k]
 
 
 def share(topo, src, dst, i, n):
@@ -82,7 +89,7 @@ def handers(topo, core, partner):
 
 
 def host_tables(near, far):
-    return [(near[0], 0, 0, L), (far[0], 1, 0, L), (near[1], 2, 0, LA), (far[1], 2, LA, L)]
+    return [(near[1], 0, 0, L), (near[0], 1, 0, L), (far[0], 2, 0, LA), (far[1], 2, LA, L)]
 
 
 def u8(v):
@@ -92,34 +99,29 @@ def u8(v):
 def hand_on(g, core, T, topo, home, near, far):
     rank = T.rank_of(home)
     mates = [T.cores[rank ^ s] for s in STEP]
-    sent = 0
+    sent, whole = 0, len(share(topo, home, core, 0, 1))
     for i, (c, k, a, e) in enumerate(host_tables(near, far)):
         if c == core:
             g.wait_ge(T.sem.rh, len(share(topo, home, core, i, 4)))
             sent += send(g, core, T, topo, [(mates[k], T.hr[:, a:e], T["hq%d" % k][:, a:e], "h%d" % k)], 1)
-    if core in (near[0], far[0]):
-        a, e = PARTS[0 if core == near[0] else 1]
-        for k in range(3):
-            g.wait_ge(T.sem["rc%d" % k], len(share(topo, home, core, 0, 1)))
+    for k in range(3):
+        if core in (near[0], far[0]):
+            a, e = PARTS[0 if core == near[0] else 1]
+            g.wait_ge(T.sem["rc%d" % k], whole)
             sent += send(g, core, T, topo, [(mates[k], u8(T["ca%d" % k][:, 0:e - a]), u8(T["rc%d" % k][:, a:e]), "c%d" % k)], 1)
-    else:
-        i = 0 if core == near[1] else 1
-        g.wait_ge(T.sem.rz, len(share(topo, home, core, i, 2)))
-        for k in range(3):
-            if not i:
-                g.wait_ge(T.sem["rc%d" % k], len(share(topo, home, core, 0, 1)))
-                sent += send(g, core, T, topo, [(mates[k], T["sa%d" % k][:, :], T["rs%d" % k][:, :], "c%d" % k)], 1)
-            if k < 2:
-                g.wait_ge(T.sem["rb%d" % k], len(share(topo, home, core, i, 2)))
-                base = 128 * (k + 1)
-            else:
-                g.wait_ge(T.sem["rb%d" % k], 2 * len(share(topo, home, core, 0, 4)))
-                base = 512
-            parts = []
-            for m in (2 * i, 2 * i + 1):
-                a = base - 32 * m
-                parts.append((mates[k], T.lb[a:a + 128, :], T["bb%d" % k][:, 2 * L * m:2 * L * (m + 1)], ("bz%d" if i else "ba%d") % k))
-            sent += send(g, core, T, topo, parts, 2)
+        elif core == near[1]:
+            g.wait_ge(T.sem["rm%d" % k], whole)
+            a, b = (T["vr%d" % k], T["rv%d" % k]) if k else (T.br, T.bb)
+            sent += send(g, core, T, topo, [(mates[k], a[:, :], b[:, :], "m%d" % k)], 1)
+        else:
+            g.wait_ge(T.sem["rc%d" % k], whole)
+            sent += send(g, core, T, topo, [(mates[k], T["sa%d" % k][:, :], T["rs%d" % k][:, :], "c%d" % k)], 1)
+            if k == 0:
+                g.wait_ge(T.sem.rg, whole)
+                sent += send(g, core, T, topo, [(mates[j], T.gr[:, :], T["gt%d" % j][:, :], "g%d" % j) for j in (1, 2)], 2)
+            if k == 2:
+                g.wait_ge(T.sem.rl, whole)
+                sent += send(g, core, T, topo, [(mates[k], T.pr[:, :], T.rp[:, :], "pl")], 1)
     g.wait_ge(T.sem.sent, sent)
 
 
@@ -135,6 +137,7 @@ def rank_program(g, core, T, topo):
     A, AF = AluOpType, ActivationFunctionType
     mates = [T.cores[rank ^ s] for s in STEP]
     near, far = handers(topo, core, mates[0])
+    backs = [handers(topo, m, core) for m in mates]
     queue = {"ve": g.vector, "se": g.scalar, "pe": g.tensor, "gp": g, "sy": g.sync}
     count, seen, sent = {"ve": 0, "se": 0, "pe": 0, "gp": 0}, {}, [0]
 
@@ -171,6 +174,9 @@ def rank_program(g, core, T, topo):
     def qu(q, qs, t, *deps):
         return op("ve", lambda: v.quantize_mx(q, qs, t), *deps)
 
+    def lay(out, a, f, first, *deps):
+        return op("ve", lambda: v.tensor_tensor_scan(out, a, f, first, A.max, A.add), *deps)
+
     def act(out, a, *deps, scale=1.0):
         if scale == 1.0:
             return op("se", lambda: s.activation(out, a, AF.Copy), *deps)
@@ -182,55 +188,86 @@ def rank_program(g, core, T, topo):
     def out_to(parts, n):
         sent[0] += send(g, core, T, topo, parts, n)
 
-    g.sync.dma_start(T.htj[:, :], T.ht[:, :]).then_inc(T.sem.dn, 16)
-    g.sync.dma_start(T.ut[:, :], T.u[:, :]).then_inc(T.sem.du, 16)
-    g.sync.dma_start(T.xt0[:, :], T.x[:, :]).then_inc(T.sem.dx, 16)
-    for d in range(2):
-        w = 16 * (d + 1)
-        g.sync.dma_start(T.hti[w:128, L * d:L * d + L], T.ht[0:128 - w, :]).then_inc(T.sem.dh, 16)
-        g.sync.dma_start(T.hti[0:w, L * d:L * d + L], T.ht[128 - w:128, :]).then_inc(T.sem.dh, 16)
-    for i in range(16):
-        a = i % 8
-        g.scalar.dma_start(T.glc[:, 88 * i:88 * i + 88], T.gl[16 * a:16 * a + 16, :]).then_inc(T.sem.dg, 16)
-    need("sy", ("dg", 256))
-    for i in range(16):
-        a = i // 2
-        g.sync.dma_start(T.eo[8 * i:8 * i + 8, :], T.glc[:, 88 * a:88 * a + 88 * SLOTS]).then_inc(T.sem.de, 16)
+    def bank(i, n):
+        return T.ps[:, BANK * i:BANK * i + n]
 
     def iota(ap, pat, base, cm, f=False):
         if f:
             return op("gp", lambda: g.iota(ap, pat, base, cm, allow_small_or_imprecise_dtypes=True))
         return op("gp", lambda: g.iota(ap, pat, base, cm))
-    k_zb = ms(T.zb[:, :], 0.0)
-    k_et = ms(T.et[:, :], 0.0)
-    k_one = ms(T.idn1[:, :], 1.0)
-    k_hlf = ms(T.hlf[:, :], 0.5)
-    k_bc = ms(T.bc[:, :], -2.0 ** -110)
+
+    g.sync.dma_start(T.htj[:, :], T.ht[:, :]).then_inc(T.sem.dn, 16)
+    g.scalar.dma_start(T.ut[:, :], T.u[:, :]).then_inc(T.sem.du, 16)
+    for i, (a, e) in enumerate(PARTS):
+        (g.sync, g.scalar)[i].dma_start(T.xt0[:, 4 * a:4 * e], T.x[:, 4 * a:4 * e]).then_inc(T.sem["dx%d" % i], 16)
+    for d in range(2):
+        w = 16 * (d + 1)
+        g.sync.dma_start(T.hti[w:128, L * d:L * d + L], T.ht[0:128 - w, :]).then_inc(T.sem.dh, 16)
+        g.sync.dma_start(T.hti[0:w, L * d:L * d + L], T.ht[128 - w:128, :]).then_inc(T.sem.dh, 16)
+    for h in range(2):
+        g.sync.dma_start(T.gd[2:10, 32 * L * h:32 * L * (h + 1)], T.gl[:, :]).then_inc(T.sem.dg, 16)
+        g.sync.dma_start(T.gd[0:2, 32 * L * h:32 * L * (h + 1)], T.gl[96:128, :]).then_inc(T.sem.dg, 16)
+    need("sy", ("dg", 64))
+    for d in range(2):
+        g.sync.dma_start(T.eo[:, 4 * L * d:4 * L * (d + 1)], T.gd[1 - d:9 - d, :]).then_inc(T.sem.de, 16)
+
     g_pc = iota(T.pc[:, :], [[1, 1]], 0, 1)
     g_uo = iota(T.uoi[:, :], [[-16, 2], [16, 8]], 112, 0)
-    g_jm = iota(T.jm[:, :], [[0, L], [1, 16]], 0, 0, True)
-    need("gp", k_zb)
-    out_to([(near[1], T.zb[:, :], T.lb[0:128, :], "rz"), (far[1], T.zb[:, :], T.lb[0:128, :], "rz")], 2)
-    k_p15 = ts(T.pi[:, 0:1], T.pc[:, :], 15, None, A.bitwise_and, deps=(g_pc,))
-    k_h = ts(T.pi[:, 1:2], T.pc[:, :], 3, 1, A.logical_shift_right, A.bitwise_and)
+    g_ji = iota(T.ji[:, :], [[1, 16]], 128, -1)
+    g_jv = iota(T.jv[:, :], [[0, 2], [16, L]], 0, 0, True)
+    k_et = ms(T.et[:, :], 0.0)
+    k_one = ms(T.idn1[:, :], 1.0)
+    k_bc = ms(T.bc[:, :], -2.0 ** -110)
+    k_p = ts(T.pi[:, 0:1], T.pc[:, :], 15, None, A.bitwise_and, deps=(g_pc,))
+    k_p = ts(T.pi[:, 1:2], T.pc[:, :], 3, 1, A.logical_shift_right, A.bitwise_and)
+    k_p = ts(T.pi[:, 2:3], T.pc[:, :], 4, None, A.logical_shift_right)
     k_uo = ts(T.uoj[:, :], T.uoi[:, :], 127, None, A.bitwise_and, deps=(g_uo,))
-    k_pf = cp(T.pf[:, 0:2], T.pi[:, 0:2], k_p15, k_h)
+    k_jr = ts(T.jr[:, :], T.ji[:, :], 15, None, A.bitwise_and, deps=(g_ji,))
+    k_pf = cp(T.pf[:, 0:3], T.pi[:, 0:3], k_p)
     k_uu = cp(T.uou[:, :], T.uoj[:, :], k_uo)
-    k_nh = ts(T.pf[:, 2:3], T.pf[:, 1:2], -1.0, 1.0, A.mult, A.add, deps=(k_pf,))
-    k_mask = ts(T.mask[:, :], T.jm[:, :], T.pf[:, 0:1], None, A.is_equal, deps=(g_jm, k_pf))
-    k_keep = ts(T.keep[:, :], T.jm[:, :], T.pf[:, 0:1], None, A.not_equal)
+    k_f = ts(T.f1[:, 0:16], T.jr[:, :], 0.0, K, A.is_equal, A.mult, deps=(k_jr,))
+    k_f = ts(T.f1[:, 16:32], T.jr[:, :], 15.0, -2 * K, A.is_equal, A.mult)
+    k_per = ts(T.per[:, :], T.jv[:, 0:L], 0.0, T.pf[:, 0:1], A.mult, A.add, deps=(g_jv, k_pf))
+    k_f = tt(T.f3[:, :], T.f1[:, 0:16], T.f1[:, 16:32], A.add, k_f)
     k_htn = cp(T.htn[:, :], T.htj[:, :], ("dn", 16))
-    m2 = cp(T.mask2[:, :], T.mask[:, :], k_mask)
-    m2 = ms(T.mask2[0:16, :], 0.0, m2)
+    k_fw = act(T.fw[:, :], T.f3[:, :].indirect(T.per[:, :]), k_f, k_per)
     k_u = qu(T.uq[:, :], T.us[:, :], T.ut[:, :], ("du", 16))
     k_up = cp(T.uqp[:, :].bitcast(dt.uint32), T.uq[:, :].bitcast(dt.uint32).indirect(T.uou[:, :]), k_u, k_uu)
     k_us = act(T.usp[:, :], T.us[:, :].indirect(T.uou[:, :]), k_u, k_uu)
     need("gp", k_htn)
     out_to([(c, T.htn[:, :], T.hr[:, :], "rh") for c, _, _, _ in host_tables(near, far)], 4)
 
-    xtok, pdread, addread = [[("dx", 16)], [("dx", 16)]], [], []
+    def tables(k, *deps):
+        gt, d, e = T["gt%d" % k], T["dtab%d" % k], T["etab%d" % k]
+        t = [None]
+
+        def s0():
+            t[0] = cp(T.gf[:, :], gt[:, :], *deps)
+
+        def s1():
+            t[0] = tt(d[:, :], T.gf[:, 2 * L:4 * L], T.gf[:, 0:2 * L], A.subtract, t[0])
+
+        def s2():
+            t[0] = ts(T.kd[:, :], d[:, :], T.cw[:, 1:2], None, A.mult, deps=(t[0],))
+
+        def s3():
+            t[0] = tt(e[:, :], T.kd[:, :], T.gf[:, 0:2 * L], A.add, t[0])
+            tab[k] = t[0]
+        return [s0, s1, s2, s3]
+
+    def guests(k):
+        return ("g%d" % k, len(share(topo, backs[k][1][1], core, 0, 2)))
+
+    def step(o, win, off, c, tok, h=LA):
+        r = []
+        if h:
+            r.append(cp(o[:, 0:16 * h], win[:, :].indirect(off[:, c:c + h]), tok))
+        r.append(act(o[:, 16 * h:C], win[:, :].indirect(off[:, c + h:c + L]), tok))
+        return r
+
+    xtok, ytok, psfree, tab = [[("dx0", 16)], [("dx1", 16)]], None, [], {}
     for k in range(4):
-        xt, xq, xs = T["xt%d" % k], T["xq%d" % k], T["xs%d" % k]
+        xt, xb, xq, xs = T["xt%d" % k], T["xb%d" % (k % 2)], T["xq%d" % k], T["xs%d" % k]
         q0 = []
         for i, (a, e) in enumerate(PARTS):
             q0.append(qu(xq[:, a:e], xs[:, a:e], xt[:, 4 * a:4 * e], xtok[i]))
@@ -239,145 +276,190 @@ def rank_program(g, core, T, topo):
                 out_to([((near[0], far[0])[i], u8(xq[:, a:e]), u8(T["ca%d" % k][:, 0:e - a]), "rc%d" % k)], 1)
         if k == 3:
             break
-        rc, rs, bl, bb, hq = T["rc%d" % k], T["rs%d" % k], T["bl%d" % k], T["bb%d" % k], T["hq%d" % k]
-        zt, zq, zs, xn = T["zt%d" % k], T["zq%d" % k], T["zs%d" % k], T["xt%d" % (k + 1)]
-        back = handers(topo, mates[k], core)
-        out_to([(near[1], xs[:, :], T["sa%d" % k][:, :], "rc%d" % k)], 1)
+        rc, rs, hq, vl = T["rc%d" % k], T["rs%d" % k], T["hq%d" % k], T["vl%d" % k]
+        zt, zq, zs, xn, yn = T["zt%d" % k], T["zq%d" % k], T["zs%d" % k], T["xt%d" % (k + 1)], T["xb%d" % ((k + 1) % 2)]
+        back = backs[k]
+        out_to([(far[1], xs[:, :], T["sa%d" % k][:, :], "rc%d" % k)], 1)
         if k == 0:
             g_id = op("gp", lambda: g.affine_select(T.idn[:, :], T.idn1[:, :], [[-1, 128]], A.is_equal, 0.0, 0, 1), k_one)
-            k_hto = cp(T.hto[:, :], T.hti[:, :], ("dh", 64))
-        sgn = []
-        for d in range(2):
-            m = mm(T.pd[:, 512 * d:512 * d + C], T.uqp[:, 128 * d:128 * d + 128], T.usp[:, 128 * d:128 * d + 128], xq[:, :], xs[:, :], q0, k_up, k_us, pdread)
-            need("se", m, k_bc)
-            sgn.append(op("se", lambda d=d: s.activation(T.sg[:, C * d:C * d + C], T.pd[:, 512 * d:512 * d + C], AF.Sign, bias=T.bc[:, 0:1])))
-        k64 = act(T.x64[:, :], xt[:, :], xtok, scale=64.0)
-        gs = [tt(T.gm[:, C * d:C * d + C], T.sg[:, C * d:C * d + C].indirect(T.hto[:, L * d:L * d + L]), T.mask[:, :], A.mult, sgn[d], k_hto, k_mask) for d in range(2)]
-        sc = [op("ve", lambda d=d: v.tensor_tensor_scan(T.sc[:, C * d:C * d + C], T.keep[:, :], T.gm[:, C * d:C * d + C], 0.0, A.mult, A.add), gs[d], k_keep) for d in range(2)]
-        k_bl = cp(bl[:, :], T.sc[:, 15:2 * C:16], sc)
-        need("gp", k_bl)
-        if k < 2:
-            a = 128 * (k + 1)
-            out_to([(c, bl[:, :], T.lb[a:a + 128, :], "rb%d" % k) for c in (near[1], far[1])], 2)
-        else:
-            out_to([(c, bl[:, :], T.lb[a:a + 128, :], "rb%d" % k) for a in (384, 512) for c in (near[1], far[1])], 4)
-        if k == 0:
-            g_jv = iota(T.jv[:, :], [[0, SLOTS], [16, L]], 0, 0, True)
-            g_mh = op("gp", lambda: g.affine_select(T.mh[:, :], T.hlf[:, :], [[-16, SLOTS], [0, L]], A.is_ge, 0.0, -16, 1), k_hlf)
             g_rm = iota(T.ramp[:, :], [[1, C]], 0, 0, True)
-            ec = [cp(T.et[:, 512 * b + b:512 * b + 512:4], T.idn[:, :], k_et, g_id) for b in range(4)]
-            a0 = ts(T.a0[:, :], T.mask[:, :], -1000.0, None, A.mult)
-            a0 = ts(T.a0[0:16, :], T.jm[0:16, :], 0.0, 16.0, A.is_equal, A.mult, deps=(a0,))
-            a0 = ms(T.a0[0:16, 0:1], 0.0, a0)
-            i0 = ms(T.ini[:, :], 0.0)
-            k_eq = qu(T.eq[:, :], T.es[:, :], T.et[:, :], ec)
-            i0 = cp(T.ini[0:16, :], T.pf[0:16, 0:1], i0)
-            k_static = [m2, a0, i0]
-            mh = ms(T.mh[0:16, :], 0.5, g_mh)
-            jp = ts(T.jp[:, :], T.jv[:, :], T.pf[:, 0:1], None, A.add, deps=(g_jv,))
-            mc = ts(T.mc[:, :], T.mh[:, :], -2.0, 1.0, A.mult, A.add, deps=(mh,))
-            ji = tt(T.ji[:, :], T.jp[:, :], T.mc[:, :], A.mult, jp, mc)
-            e1 = ts(T.t1[:, :], T.eo[:, 0:88 * SLOTS:2], T.pf[:, 2:3], None, A.mult, deps=(("de", 256), k_nh))
-            e2 = ts(T.t2[:, :], T.eo[:, 1:88 * SLOTS:2], T.pf[:, 1:2], None, A.mult)
-            e3 = tt(T.sel[:, :], T.t1[:, :], T.t2[:, :], A.add, e1, e2)
-            for d in range(SLOTS):
-                c = 44 * (SLOTS - 1 - d)
-                ee, oo = T.sel[:, c:c + L], T.sel[:, c + L:c + 2 * L]
-                sm = tt(T.sm[:, L * d:L * d + L], ee, oo, A.add, e3)
-                df = tt(T.df[:, L * d:L * d + L], oo, ee, A.subtract)
-            em = tt(T.em[:, :], T.sm[:, :], T.mh[:, :], A.mult, sm)
-            dtb = tt(T.dtab[:, :], T.df[:, :], T.mh[:, :], A.mult, df)
-            etb = tt(T.etab[:, :], T.em[:, :], T.ji[:, :], A.add, em, ji)
-            k_tab = [dtb, etb]
-        call = ("c%d" % k, sum(len(share(topo, c, core, 0, 1)) for c in (back[0][0], back[1][0], back[0][1])))
+            k_hto = cp(T.hto[:, :], T.hti[:, :], ("dh", 64))
+        sa, sb = [], []
+        for i, (a, e) in enumerate(PARTS):
+            m = [mm(bank(4 * i + d, e - a), T.uqp[:, 128 * d:128 * d + 128], T.usp[:, 128 * d:128 * d + 128], xq[:, a:e], xs[:, a:e], q0[i], k_up, k_us, psfree) for d in range(2)]
+            sa.append(ts(T.sg[:, a:e], bank(4 * i, e - a), 0.0, 0.5, A.is_gt, A.subtract, deps=(m[0],)))
+            need("se", m[1], k_bc)
+            sb.append(op("se", lambda i=i, a=a, e=e: s.activation(T.sg[:, C + a:C + e], bank(4 * i + 1, e - a), AF.Sign, bias=T.bc[:, 0:1])))
+        ga = cp(T.gm[:, 0:C], T.sg[:, 0:C].indirect(T.hto[:, 0:L]), sa, k_hto)
+        gb = act(T.gm[:, C:2 * C], T.sg[:, C:2 * C].indirect(T.hto[:, L:2 * L]), sb, k_hto, scale=0.5)
+        sc = [lay(T.sc[:, C * d:C * d + C], T.gm[:, C * d:C * d + C], T.fw[:, :], -K, (ga, gb)[d], k_fw) for d in range(2)]
+        psfree = psfree + sa + sb
+        call = ("c%d" % k, sum(len(share(topo, c, core, 0, 1)) for c in (back[0][0], back[1][0], back[1][1])))
+        msg = ("m%d" % k, len(share(topo, back[0][1], core, 0, 1)))
+        hs = ("h%d" % k, sum(len(share(topo, c, core, 0, 1)) for c, kk, _, _ in host_tables(*back) if kk == k))
+        dc, lg = [], []
+
+        def unpack(b):
+            i = (2, 3, 6, 7)[b]
+            m = mm(bank(i, C), T.eq[:, 128 * b:128 * b + 128], T.es[:, 128 * b:128 * b + 128], rc[:, :], rs[:, :], call, k_eq, addread)
+            dc.append(act(T.ds[:, C * b:C * b + C], bank(i, C), m))
+
+        def larger(b):
+            lg.append(tt(T.mm[:, C * b:C * b + C], T.ds[:, C * b:C * b + C].indirect(hq[:, :]), xt[:, b:4 * C:4], A.max, dc[b], hs))
+
+        def lists(src, *deps):
+            n = tt(T.nt[:, :], src, T["dtab%d" % k][:, :], A.mult, tab[k], *deps)
+            n = tt(T.nf[:, :], T.nt[:, :], T["etab%d" % k][:, :], A.add, n)
+            return cp(T.nu[:, :], T.nf[:, :], n)
+
+        def rest(t2):
+            c = lay(T.sp[:, :], T.yb[:, :], T.fv[:, :], T.iv[:, 0:1], t2, k_static)
+
+            def on(e, a, w):
+                return ts(T.slot[a + 32 * e:a + 32 * e + w, L * e:L * e + L], T.sp[a:a + w, 15:C:16], T.cv[a:a + w, 0:1], None, A.add, deps=(c,))
+            c1 = [on(1, a, 32) for a in (0, 32, 64)]
+            t = step(T.ya, T.yb, T.slot, L, [t2, c1])
+            c2 = on(2, 0, 64)
+            c3 = on(3, 0, 32)
+            t = step(T.yb, T.ya, T.slot, 2 * L, [t, c2])
+            t = step(T.ya, T.yb, T.slot, 3 * L, [t, c3])
+            c = lay(T.sv[:, :], T.ya[:, :], T.fv[:, :], T.iv[:, 0:1], t)
+            return t, ts(vl[:, :], T.sv[:, 15:C:16], T.cv[:, 0:1], None, A.add, deps=(c,))
+
         if k == 0:
+            k_bl = cp(T.bl[:, :], T.sc[:, 15:2 * C:16], sc)
+            need("gp", k_bl)
+            out_to([(near[1], T.bl[:, :], T.br[:, :], "rm0")], 1)
+            ytok = [act(xb[:, :], xt[:, :], xtok, scale=64.0)]
+            ec = [cp(T.et[:, 512 * b + b:512 * b + 512:4], T.idn[:, :], k_et, g_id) for b in range(4)]
+            c0 = ts(T.pf[:, 3:4], T.pf[:, 1:2], -1.0, 1.0, A.mult, A.add, deps=(k_pf,))
+            c0 = ts(T.pf[:, 4:5], T.pf[:, 2:3], 1.0, None, A.not_equal)
+            c0 = ts(T.pf[:, 5:6], T.pf[:, 2:3], 1.0, None, A.is_equal)
+            c0 = ts(T.pf[:, 6:7], T.pf[:, 0:1], 0.0, 2 * K, A.is_equal, A.mult)
+            jp = ts(T.jp[:, :], T.jv[:, :], T.pf[:, 0:1], None, A.add)
+            k_eq = qu(T.eq[:, :], T.es[:, :], T.et[:, :], ec)
+            e1 = ts(T.t1[:, :], T.eo[:, 0:8 * L:2], T.pf[:, 3:4], None, A.mult, deps=(("de", 32), c0))
+            e2 = ts(T.t2[:, :], T.eo[:, 1:8 * L:2], T.pf[:, 1:2], None, A.mult)
+            jm = ts(T.jm[:, :], T.jp[:, :], T.pf[:, 5:6], None, A.mult, deps=(jp,))
+            cw = ts(T.cw[:, 0:1], T.pf[:, 6:7], -K, None, A.add)
+            cv = ts(T.cv[:, :], T.pf[:, 6:7], -K, None, A.add)
+            ck = ts(T.cw[:, 1:2], T.pf[:, 6:7], 0.5 - K, None, A.add)
+            e3 = tt(T.sel[:, :], T.t1[:, :], T.t2[:, :], A.add, e1, e2)
+            f4 = cp(T.f4[:, :], T.f3[:, :])
+            iv = ms(T.iv[:, :], -K)
+            sl = [cp(T.slot[:, 2 * L * i:2 * L * (i + 1)], T.jp[:, :]) for i in range(2)]
+            e4 = ts(T.selb[:, :], T.sel[:, 2 * L:4 * L], T.pf[:, 4:5], None, A.mult, deps=(e3,))
+            f4 = ms(T.f4[0:16, :], 0.0, f4)
+            cv = ms(T.cv[0:16, :], -K, cv)
+            iv = ts(T.iv[0:16, :], T.pf[0:16, 0:1], K - 16, None, A.add, deps=(iv,))
+            e5 = tt(T.selc[:, :], T.selb[:, :], T.jm[:, :], A.add, e4, jm)
+            f4 = ms(T.f4[0:16, 0:1], 16.0, f4)
+            e6 = [cp(T.gt0[:, 2 * L * i:2 * L * i + L], T.sel[:, L * i:L * i + L]) for i in range(2)]
+            e6 += [cp(T.gt0[:, 2 * L * i + L:2 * L * (i + 1)], T.selc[:, L * i:L * i + L], e5) for i in range(2)]
+            k_fv = act(T.fv[:, :], T.f4[:, :].indirect(T.per[:, :]), f4)
+            k_static = [k_fv, cw, cv, iv, sl]
+            need("gp", e6)
+            out_to([(far[1], T.gt0[:, :], T.gr[:, :], "rg")], 1)
+            for f in tables(0, e6, ck):
+                f()
             need("sy", call)
             g.sync.dma_start(u8(T.wq[:, :]), T.wc[:, :]).then_inc(T.sem.dw, 16)
             g.sync.dma_start(T.wsc[:, :], T.ws[:, :]).then_inc(T.sem.dw, 16)
             g.sync.dma_start(T.vt[:, :], T.v[:, :]).then_inc(T.sem.dv, 16)
-        dc = []
-        for b in range(4):
-            m = mm(T.pd[:, 512 * b:512 * b + C], T.eq[:, 128 * b:128 * b + 128], T.es[:, 128 * b:128 * b + 128], rc[:, :], rs[:, :], call, k_eq, sgn)
-            dc.append(act(T.ds[:, C * b:C * b + C], T.pd[:, 512 * b:512 * b + C], m))
-        pdread = dc
-        hs = ("h%d" % k, sum(len(share(topo, c, core, 0, 1)) for c, kk, _, _ in host_tables(*back) if kk == k))
-
-        def larger(b):
-            return tt(T.mm[:, C * b:C * b + C], T.ds[:, C * b:C * b + C].indirect(hq[:, :]), xt[:, b:4 * C:4], A.max, dc[b], hs)
-
-        def lists(a, e, *deps):
-            n1 = tt(T.nt[:, a:e], bb[:, a:e], T.dtab[:, a:e], A.mult, k_tab, *deps)
-            n2 = tt(T.nf[:, a:e], T.nt[:, a:e], T.etab[:, a:e], A.add, n1)
-            return cp(T.nu[:, a:e], T.nf[:, a:e], n2)
-        ba = ("ba%d" % k, 2 * len(share(topo, back[0][1], core, 0, 2)))
-        bz = ("bz%d" % k, 2 * len(share(topo, back[1][1], core, 0, 2)))
-        lg = [larger(b) for b in range(3)]
-        n1 = lists(0, 2 * L, ba)
-        n2 = lists(2 * L, L * SLOTS, bz)
-        lg += [larger(3)]
-        win, tok, ys = T.ramp, [g_rm], [T.ya, T.yb]
-        for d in range(6):
-            o, n = ys[d % 2], n1 if d < 2 else n2
-            c = L * d
-            if d < 2:
-                tok = [act(o[:, :], win[:, :].indirect(T.nu[:, c:c + L]), tok, n)]
+            addread = []
+            for b in range(4):
+                unpack(b)
+            larger(0)
+            larger(1)
+            n = lists(T.bb[:, :], msg)
+            t = step(T.ya, T.ramp, T.nu, 0, [n, g_rm], 0)
+            larger(2)
+            t = step(T.yb, T.ya, T.nu, L, [t], 0)
+            larger(3)
+            t, k_vl = rest(t)
+            mine = vl
+        else:
+            n = lists(T.sc[:, 15:2 * C:16], sc)
+            t = step(T.ya, T.ramp, T.nu, 0, [n])
+            t = step(T.yb, T.ya, T.nu, L, [t])
+            t, c = rest(t)
+            need("gp", c)
+            out_to([(near[1], vl[:, :], T["vr%d" % k][:, :], "rm%d" % k)], 1)
+            for b in range(4):
+                unpack(b)
+            if k == 2:
+                c6 = cp(T.slot[0:16, 0:L], vl[96:112, :], c)
+                c7 = cp(T.l2[:, :], vl[:, :])
+            for b in range(4):
+                larger(b)
+            if k == 1:
+                for f in tables(2, guests(2)):
+                    f()
             else:
-                h = 16 * LA
-                tok = [cp(o[:, 0:h], win[:, :].indirect(T.nu[:, c:c + LA]), tok, n), act(o[:, h:C], win[:, :].indirect(T.nu[:, c + LA:c + L]), tok, n)]
-            win = o
-        c6 = tt(T.mk2[:, :], win[:, :].indirect(T.nu[:, 6 * L:7 * L]), T.mask2[:, :], A.mult, tok, k_static)
-        c7 = op("ve", lambda: v.tensor_tensor_scan(T.sc2[:, :], T.a0[:, :], T.mk2[:, :], T.ini[:, 0:1], A.add, A.max), c6)
-        k_vl = cp(T.vl[:, :], T.sc2[:, 15:C:16], c7)
+                t8 = act(T.yb[:, :], T.ya[:, :].indirect(T.slot[:, 0:L]), t, c6)
+                c8 = lay(T.sp[:, :], T.yb[:, :], T.fw[:, :], -K, t8)
+                c9 = ts(T.l2[0:16, :], T.sp[0:16, 15:C:16], T.cw[0:16, 0:1], None, A.add, deps=(c8, c7))
+                need("gp", c9)
+                out_to([(far[1], T.l2[:, :], T.pr[:, :], "rl")], 1)
+            k_vl, mine = msg, T["rv%d" % k]
+        psfree = psfree + dc
         zc = [[], []]
 
         def mosaic(i, b, e):
             a, z = PARTS[i]
-            o, w = zt[:, 4 * a + b:4 * z:4], T.mm[:, C * b:C * b + C].indirect(T.vl[:, a // 16:z // 16])
+            o, w = zt[:, 4 * a + b:4 * z:4], T.mm[:, C * b:C * b + C].indirect(mine[:, a // 16:z // 16])
             zc[i].append(cp(o, w, k_vl, lg) if e == "ve" else act(o, w, k_vl, lg))
-        for i, b, e in ((0, 0, "ve"), (0, 2, "se"), (0, 1, "ve"), (0, 3, "se"), (1, 0, "ve"), (1, 2, "se"), (1, 3, "se"), (1, 1, "se")):
-            mosaic(i, b, e)
-        if k == 2:
-            o = ys[0]
-            t6 = act(o[:, :], win[:, :].indirect(T.nu[:, 6 * L:7 * L]), tok)
-        xtok = [[], []]
+
+        xtok, ynew = [[], []], []
 
         def layer(i):
             a, z = PARTS[i]
             qz = qu(zq[:, a:z], zs[:, a:z], zt[:, 4 * a:4 * z], zc[i])
-            ps = (T.pw, T.pd)[i]
-            return [mm(ps[:, 512 * b:512 * b + z - a], T.wq[:, 128 * b:128 * b + 128], T.wsc[:, 128 * b:128 * b + 128], zq[:, a:z], zs[:, a:z], qz, ("dw", 32), pdread, addread) for b in range(4)]
+            return [mm(bank(4 * i + b, z - a), T.wq[:, 128 * b:128 * b + 128], T.wsc[:, 128 * b:128 * b + 128], zq[:, a:z], zs[:, a:z], qz, ("dw", 32), psfree) for b in range(4)]
 
         def state(i, b, m):
             a, z = PARTS[i]
-            ps = (T.pw, T.pd)[i]
-            ad = tt(T.tf[:, C * b + a:C * b + z], ps[:, 512 * b:512 * b + z - a], T.x64[:, 4 * a + b:4 * z:4], A.add, m, k64)
-            xtok[i].append(act(xn[:, 4 * a + b:4 * z:4], T.tf[:, C * b + a:C * b + z], ad, scale=2.0 ** -6))
-            return ad
+            ad = tt(yn[:, 4 * a + b:4 * z:4], bank(4 * i + b, z - a), xb[:, 4 * a + b:4 * z:4], A.add, m, ytok)
+            xtok[i].append(act(xn[:, 4 * a + b:4 * z:4], yn[:, 4 * a + b:4 * z:4], ad, scale=2.0 ** -6))
+            ynew.append(ad)
+        for i, b, e in ((0, 0, "ve"), (0, 2, "se"), (0, 1, "ve"), (0, 3, "se"), (1, 2, "se"), (1, 3, "se"), (1, 1, "se")):
+            mosaic(i, b, e)
         ma = layer(0)
+        mosaic(1, 0, "ve")
+        extra = tables(1, guests(1)) if k == 0 else []
+        for b in range(2):
+            state(0, b, ma[b])
         mb = layer(1)
-        addread = [state(0, b, ma[b]) for b in range(4)] + [state(1, b, mb[b]) for b in range(4)]
-        pdread = pdread + addread
-        if k == 0:
+        for b in range(2, 4):
+            state(0, b, ma[b])
+        for b in range(4):
+            state(1, b, mb[b])
+            if extra:
+                extra[b]()
+        ytok = addread = ynew
+        psfree = psfree + ynew
+        if k == 1:
             k_v = qu(T.vq[:, :], T.vs[:, :], T.vt[:, :], ("dv", 16))
-        if k == 2:
-            pltok = act(T.plr[:, :], ys[0][:, :].indirect(T.nu[:, 7 * L:8 * L]), t6)
 
     do = [0]
 
-    def store(out, a, *deps):
-        need("sy", *deps)
-        g.sync.dma_start(out, a).then_inc(T.sem.do, 16)
+    def store(e, out, a, *deps):
+        need(e, *deps)
+        queue[e].dma_start(out, a).then_inc(T.sem.do, 16)
         do[0] += 16
     yc = []
     for i, (a, e) in enumerate(PARTS):
-        m = mm(T.pd[:, 512 * i:512 * i + e - a], T.vq[:, :], T.vs[:, :], T.xq3[:, a:e], T.xs3[:, a:e], q0[i], k_v, pdread)
-        yc.append(cp(T.yt[:, a:e], T.pd[:, 512 * i:512 * i + e - a], m) if i else act(T.yt[:, a:e], T.pd[:, 0:e - a], m))
-    store(T.oc[:, :], u8(T.xq3[:, :]), q0)
+        m = mm(bank(4 * i, e - a), T.vq[:, :], T.vs[:, :], T.xq3[:, a:e], T.xs3[:, a:e], q0[i], k_v, psfree)
+        yc.append(cp(T.yt[:, a:e], bank(4 * i, e - a), m))
+    pltok = act(T.plr[:, :], T.ramp[:, :].indirect(T.rp[:, :]), ("pl", len(share(topo, backs[2][1][1], core, 0, 1))))
+    for i, (a, e) in enumerate(PARTS):
+        store("sy", T.oc[:, 4 * a:4 * e], u8(T.xq3[:, a:e]), q0[i])
     for b in range(4):
-        store(T.osc[4 * b:4 * b + 4, :], T.xs3[32 * b:32 * b + 4, :])
-    store(T.y[:, :], T.yt[:, :], yc)
-    store(T.pl[0:7, :], T.plr[16:128:16, :], pltok)
-    store(T.pl[7:8, :], T.plr[0:1, :])
+        store("sy", T.osc[4 * b:4 * b + 4, :], T.xs3[32 * b:32 * b + 4, :])
+    store("se", T.pl[0:7, :], T.plr[16:128:16, :], pltok)
+    store("se", T.pl[7:8, :], T.plr[0:1, :])
+    for i, (a, e) in enumerate(PARTS):
+        store(("se", "sy")[i], T.y[:, a:e], T.yt[:, a:e], yc[i])
     g.sync.wait_ge(T.sem.do, do[0])
     for e in ("ve", "se", "pe", "gp"):
         need("gp", (e, count[e]))

@@ -5,10 +5,12 @@ C = 352
 STEP = [1, 2, 4]
 L = C // 16
 LA = 12
-PARTS = [(0, 16 * LA), (16 * LA, C)]
+LW = 12
 F8 = "float8_e4m3fn_x4"
-K = 512.0
+K = 1024.0
 BANK = 512
+GUEST = [(0, (0,), ()), (0, (1, 2), (0,)), (0, (3,), (1,)), (0, (), (2, 3)), (LW, (), ())]
+HOST = [(0, (), ()), (LW, (), ()), (LW, (), ()), (LW, (), ()), (LW, (0, 1, 2, 3), ())]
 
 SCRATCH = {
     "ut": ("sbuf", [128, 512], "bfloat16"), "uq": ("sbuf", [128, 128], F8), "us": ("sbuf", [128, 128], "uint8"),
@@ -16,31 +18,26 @@ SCRATCH = {
     "vt": ("sbuf", [128, 512], "bfloat16"), "vq": ("sbuf", [128, 128], F8), "vs": ("sbuf", [128, 128], "uint8"),
     "wq": ("sbuf", [128, 512], F8), "wsc": ("sbuf", [128, 512], "uint8"),
     "idn1": ("sbuf", [128, 128], "float32"), "idn": ("sbuf", [128, 128], "float32"),
-    "et": ("sbuf", [128, 2048], "bfloat16"), "eq": ("sbuf", [128, 512], F8), "es": ("sbuf", [128, 512], "uint8"),
-    "hti": ("sbuf", [128, 2 * L], "int32"), "htj": ("sbuf", [128, L], "int32"),
-    "hto": ("sbuf", [128, 2 * L], "uint16"), "htn": ("sbuf", [128, L], "uint16"),
+    "et": ("sbuf", [128, 516], "bfloat16"), "eq": ("sbuf", [128, 512], F8), "es": ("sbuf", [128, 512], "uint8"),
+    "hti": ("sbuf", [128, 2 * L], "int32"), "htj": ("sbuf", [128, L], "int32"), "hto": ("sbuf", [128, 2 * L], "uint16"),
     "gd": ("dram", [10, 64 * L], "int32"), "eo": ("sbuf", [128, 8 * L], "int32"),
     "pc": ("sbuf", [128, 1], "int32"), "pi": ("sbuf", [128, 8], "int32"), "pf": ("sbuf", [128, 8], "float32"),
-    "bc": ("sbuf", [128, 1], "float32"), "cw": ("sbuf", [128, 2], "float32"), "cv": ("sbuf", [128, 1], "float32"),
+    "bc": ("sbuf", [128, 1], "float32"), "cw": ("sbuf", [128, 4], "float32"), "cv": ("sbuf", [128, 1], "float32"),
     "iv": ("sbuf", [128, 1], "float32"), "xb0": ("sbuf", [128, 4 * C], "bfloat16"), "xb1": ("sbuf", [128, 4 * C], "bfloat16"),
-    "uoi": ("sbuf", [128, 16], "int32"), "uoj": ("sbuf", [128, 16], "int32"), "uou": ("sbuf", [128, 16], "uint16"),
-    "ji": ("sbuf", [128, 16], "int32"), "jr": ("sbuf", [128, 16], "int32"),
+    "ui": ("sbuf", [128, 32], "int32"), "uj": ("sbuf", [128, 32], "int32"), "uou": ("sbuf", [128, 16], "uint16"),
     "f1": ("sbuf", [128, 32], "float32"), "f3": ("sbuf", [128, 16], "float32"), "f4": ("sbuf", [128, 16], "float32"),
-    "ramp": ("sbuf", [128, C], "float32"), "jv": ("sbuf", [128, 2 * L], "float32"), "jp": ("sbuf", [128, 2 * L], "float32"),
-    "jm": ("sbuf", [128, 2 * L], "float32"), "per": ("sbuf", [128, L], "uint16"),
+    "ramp": ("sbuf", [128, C], "float32"), "jv": ("sbuf", [128, 2 * L], "float32"), "per": ("sbuf", [128, L], "uint16"),
     "fw": ("sbuf", [128, C], "bfloat16"), "fv": ("sbuf", [128, C], "bfloat16"),
-    "t1": ("sbuf", [128, 4 * L], "float32"), "t2": ("sbuf", [128, 4 * L], "float32"), "sel": ("sbuf", [128, 4 * L], "float32"),
-    "selb": ("sbuf", [128, 2 * L], "float32"), "selc": ("sbuf", [128, 2 * L], "float32"),
-    "gt0": ("sbuf", [128, 4 * L], "uint16"), "gf": ("sbuf", [128, 4 * L], "float32"), "kd": ("sbuf", [128, 2 * L], "float32"),
-    "sg": ("sbuf", [128, 2 * C], "bfloat16"), "gm": ("sbuf", [128, 2 * C], "bfloat16"), "sc": ("sbuf", [128, 2 * C], "float16"),
-    "bl": ("sbuf", [128, 2 * L], "float32"), "bb": ("sbuf", [128, 2 * L], "float32"),
-    "nt": ("sbuf", [128, 2 * L], "float32"), "nf": ("sbuf", [128, 2 * L], "float32"), "nu": ("sbuf", [128, 2 * L], "uint16"),
-    "ya": ("sbuf", [128, C], "float32"), "yb": ("sbuf", [128, C], "float32"), "plr": ("sbuf", [128, C], "float32"),
+    "t1": ("sbuf", [128, 8 * L], "float32"), "sel": ("sbuf", [128, 4 * L], "float32"), "gw": ("sbuf", [128, 2 * C], "float32"),
+    "sg": ("sbuf", [128, 2 * C], "bfloat16"), "ga": ("sbuf", [128, C], "float16"), "gb": ("sbuf", [128, C], "bfloat16"),
+    "sc": ("sbuf", [128, 2 * C], "float16"), "bl": ("sbuf", [128, 2 * L], "uint16"), "bb": ("sbuf", [128, 2 * L], "uint16"),
+    "nt": ("sbuf", [128, 4 * L], "float32"), "nu": ("sbuf", [128, L], "uint16"), "ul": ("sbuf", [128, L], "uint16"),
+    "ya": ("sbuf", [128, C], "float32"), "yb": ("sbuf", [128, C], "float32"),
     "sp": ("sbuf", [128, C], "float32"), "sv": ("sbuf", [128, C], "float32"), "slot": ("sbuf", [128, 4 * L], "uint16"),
-    "l2": ("sbuf", [128, L], "uint16"), "rp": ("sbuf", [128, L], "uint16"),
+    "po": ("dram", [128, L], "float32"), "pn": ("dram", [128, L], "float32"),
     "ds": ("sbuf", [128, 4 * C], "bfloat16"), "mm": ("sbuf", [128, 4 * C], "bfloat16"), "yt": ("sbuf", [128, C], "float32"),
     "ps": ("psum", [128, 8 * BANK], "float32"),
-    "hr": ("sbuf", [128, L], "uint16"), "gr": ("sbuf", [128, 4 * L], "uint16"), "br": ("sbuf", [128, 2 * L], "float32"), "pr": ("sbuf", [128, L], "uint16"),
+    "hr": ("sbuf", [128, L], "int32"), "gr": ("sbuf", [128, 4 * L], "float32"), "br": ("sbuf", [128, 2 * L], "uint16"), "pr": ("dram", [128, L], "float32"),
 }
 for _k in range(4):
     SCRATCH["xt%d" % _k] = ("sbuf", [128, 4 * C], "bfloat16")
@@ -52,29 +49,33 @@ for _k in range(3):
     SCRATCH["zt%d" % _k] = ("sbuf", [128, 4 * C], "bfloat16")
     SCRATCH["zq%d" % _k] = ("sbuf", [128, C], F8)
     SCRATCH["zs%d" % _k] = ("sbuf", [128, C], "uint8")
-    SCRATCH["hq%d" % _k] = ("sbuf", [128, L], "uint16")
     SCRATCH["vl%d" % _k] = ("sbuf", [128, L], "uint16")
-    SCRATCH["dtab%d" % _k] = ("sbuf", [128, 2 * L], "float32")
-    SCRATCH["etab%d" % _k] = ("sbuf", [128, 2 * L], "float32")
-    SCRATCH["ca%d" % _k] = ("sbuf", [128, 16 * LA], F8)
+    SCRATCH["hi%d" % _k] = ("sbuf", [128, L], "int32")
+    SCRATCH["hq%d" % _k] = ("sbuf", [128, L], "uint16")
+    SCRATCH["tab%d" % _k] = ("sbuf", [128, 4 * L], "float32")
+    SCRATCH["gt%d" % _k] = ("sbuf", [128, 2 * L], "uint16")
+    SCRATCH["ca%d" % _k] = ("sbuf", [128, C - 128], F8)
     SCRATCH["sa%d" % _k] = ("sbuf", [128, C], "uint8")
 for _k in (1, 2):
-    SCRATCH["gt%d" % _k] = ("sbuf", [128, 4 * L], "uint16")
     SCRATCH["vr%d" % _k] = ("sbuf", [128, L], "uint16")
     SCRATCH["rv%d" % _k] = ("sbuf", [128, L], "uint16")
 
-SEMAPHORES = ["ve", "se", "pe", "gp", "dx0", "dx1", "du", "dn", "dh", "dg", "dw", "dv", "de", "do", "sent", "rh", "rg", "rl", "pl"]
+SEMAPHORES = ["ve", "se", "pe", "gp", "dx0", "dx1", "du", "dn", "dh", "dg", "dw", "dv", "de", "dp", "do", "sent", "rh", "rg", "rl", "pl"]
 for _k in range(3):
     SEMAPHORES += ["c%d" % _k, "m%d" % _k, "h%d" % _k, "g%d" % _k, "rc%d" % _k, "rm%d" % _k]
+
+
+def parts():
+    return [(0, 16 * LA), (16 * LA, C)]
 
 
 def share(topo, src, dst, i, n):
     return topo.engines(src, dst)[i::n]
 
 
-def send(g, core, T, topo, parts, n):
+def send(g, core, T, topo, moves, n):
     ts, total = [], 0
-    for i, (dst, a, b, sem) in enumerate(parts):
+    for i, (dst, a, b, sem) in enumerate(moves):
         e = share(topo, core, dst, i, n)
         rid, pid = topo.addr(dst, core)
         ts.append(RemoteDMATransfer(dst_ids=[DstId(rid=rid, pnc=pid)], dma_engine_mask=sum(1 << j for j in e), remote_sem=T.sem[sem], srcs=[a], dsts=[b]))
@@ -89,7 +90,7 @@ def handers(topo, core, partner):
 
 
 def host_tables(near, far):
-    return [(near[1], 0, 0, L), (near[0], 1, 0, L), (far[0], 2, 0, LA), (far[1], 2, LA, L)]
+    return [(near[1], 0, 0, L), (near[0], 1, 0, L), (far[0], 2, 0, L // 2), (far[1], 2, L // 2, L)]
 
 
 def u8(v):
@@ -103,10 +104,10 @@ def hand_on(g, core, T, topo, home, near, far):
     for i, (c, k, a, e) in enumerate(host_tables(near, far)):
         if c == core:
             g.wait_ge(T.sem.rh, len(share(topo, home, core, i, 4)))
-            sent += send(g, core, T, topo, [(mates[k], T.hr[:, a:e], T["hq%d" % k][:, a:e], "h%d" % k)], 1)
+            sent += send(g, core, T, topo, [(mates[k], T.hr[:, a:e], T["hi%d" % k][:, a:e], "h%d" % k)], 1)
     for k in range(3):
         if core in (near[0], far[0]):
-            a, e = PARTS[0 if core == near[0] else 1]
+            a, e = parts()[0 if core == near[0] else 1]
             g.wait_ge(T.sem["rc%d" % k], whole)
             sent += send(g, core, T, topo, [(mates[k], u8(T["ca%d" % k][:, 0:e - a]), u8(T["rc%d" % k][:, a:e]), "c%d" % k)], 1)
         elif core == near[1]:
@@ -118,10 +119,10 @@ def hand_on(g, core, T, topo, home, near, far):
             sent += send(g, core, T, topo, [(mates[k], T["sa%d" % k][:, :], T["rs%d" % k][:, :], "c%d" % k)], 1)
             if k == 0:
                 g.wait_ge(T.sem.rg, whole)
-                sent += send(g, core, T, topo, [(mates[j], T.gr[:, :], T["gt%d" % j][:, :], "g%d" % j) for j in (1, 2)], 2)
+                sent += send(g, core, T, topo, [(mates[j], T.gr[:, :], T["tab%d" % j][:, :], "g%d" % j) for j in (1, 2)], 2)
             if k == 2:
                 g.wait_ge(T.sem.rl, whole)
-                sent += send(g, core, T, topo, [(mates[k], T.pr[:, :], T.rp[:, :], "pl")], 1)
+                sent += send(g, core, T, topo, [(mates[k], T.pr[:, :], T.pn[:, :], "pl")], 1)
     g.wait_ge(T.sem.sent, sent)
 
 
@@ -134,7 +135,7 @@ def rank_program(g, core, T, topo):
                 if core in near[:2] + far[:2]:
                     hand_on(g, core, T, topo, home, near, far)
         return
-    A, AF = AluOpType, ActivationFunctionType
+    A, AF, PARTS = AluOpType, ActivationFunctionType, parts()
     mates = [T.cores[rank ^ s] for s in STEP]
     near, far = handers(topo, core, mates[0])
     backs = [handers(topo, m, core) for m in mates]
@@ -185,8 +186,8 @@ def rank_program(g, core, T, topo):
     def mm(out, q, qs, x, xs, *deps):
         return op("pe", lambda: p.matmul_mx(out, q, qs, x, xs, True, True), *deps)
 
-    def out_to(parts, n):
-        sent[0] += send(g, core, T, topo, parts, n)
+    def out_to(moves, n):
+        sent[0] += send(g, core, T, topo, moves, n)
 
     def bank(i, n):
         return T.ps[:, BANK * i:BANK * i + n]
@@ -197,75 +198,73 @@ def rank_program(g, core, T, topo):
         return op("gp", lambda: g.iota(ap, pat, base, cm))
 
     g.sync.dma_start(T.htj[:, :], T.ht[:, :]).then_inc(T.sem.dn, 16)
-    g.scalar.dma_start(T.ut[:, :], T.u[:, :]).then_inc(T.sem.du, 16)
+    g.sync.dma_start(T.ut[:, :], T.u[:, :]).then_inc(T.sem.du, 16)
     for i, (a, e) in enumerate(PARTS):
-        (g.sync, g.scalar)[i].dma_start(T.xt0[:, 4 * a:4 * e], T.x[:, 4 * a:4 * e]).then_inc(T.sem["dx%d" % i], 16)
+        g.sync.dma_start(T.xt0[:, 4 * a:4 * e], T.x[:, 4 * a:4 * e]).then_inc(T.sem["dx%d" % i], 16)
     for d in range(2):
         w = 16 * (d + 1)
         g.sync.dma_start(T.hti[w:128, L * d:L * d + L], T.ht[0:128 - w, :]).then_inc(T.sem.dh, 16)
         g.sync.dma_start(T.hti[0:w, L * d:L * d + L], T.ht[128 - w:128, :]).then_inc(T.sem.dh, 16)
     for h in range(2):
-        g.sync.dma_start(T.gd[2:10, 32 * L * h:32 * L * (h + 1)], T.gl[:, :]).then_inc(T.sem.dg, 16)
-        g.sync.dma_start(T.gd[0:2, 32 * L * h:32 * L * (h + 1)], T.gl[96:128, :]).then_inc(T.sem.dg, 16)
-    need("sy", ("dg", 64))
-    for d in range(2):
-        g.sync.dma_start(T.eo[:, 4 * L * d:4 * L * (d + 1)], T.gd[1 - d:9 - d, :]).then_inc(T.sem.de, 16)
+        g.scalar.dma_start(T.gd[2:10, 32 * L * h:32 * L * (h + 1)], T.gl[:, :]).then_inc(T.sem.dg, 16)
+        g.scalar.dma_start(T.gd[0:2, 32 * L * h:32 * L * (h + 1)], T.gl[96:128, :]).then_inc(T.sem.dg, 16)
 
-    g_pc = iota(T.pc[:, :], [[1, 1]], 0, 1)
-    g_uo = iota(T.uoi[:, :], [[-16, 2], [16, 8]], 112, 0)
-    g_ji = iota(T.ji[:, :], [[1, 16]], 128, -1)
-    g_jv = iota(T.jv[:, :], [[0, 2], [16, L]], 0, 0, True)
-    k_et = ms(T.et[:, :], 0.0)
     k_one = ms(T.idn1[:, :], 1.0)
+    k_et = ms(T.et[:, :], 0.0)
+    g_pc = iota(T.pc[:, :], [[1, 1]], 0, 1)
+    g_uo = iota(T.ui[:, 0:16], [[-16, 2], [16, 8]], 112, 0)
+    g_ji = iota(T.ui[:, 16:32], [[1, 16]], 128, -1)
+    g_jv = iota(T.jv[:, :], [[0, 2], [16, L]], 0, 0, True)
+    g_eo = iota(T.eo[:, 4 * L:8 * L], [[0, 2], [16, L], [0, 2]], -16, 1)
+    g_rm = iota(T.ramp[:, :], [[1, C]], 0, 0, True)
+    need("sy", ("dg", 64), g_eo)
+    g.sync.dma_start(T.eo[:, 0:4 * L], T.gd[1:9, :]).then_inc(T.sem.de, 16)
+    g.sync.dma_start(T.eo[0:16, 4 * L:8 * L], T.gd[0:1, :]).then_inc(T.sem.de, 16)
+    g.sync.dma_start(T.eo[32:128, 4 * L:8 * L], T.gd[2:8, :]).then_inc(T.sem.de, 16)
+    need("gp", ("dn", 16))
+    out_to([(c, T.htj[:, :], T.hr[:, :], "rh") for c, _, _, _ in host_tables(near, far)], 4)
+    g_id = op("gp", lambda: g.affine_select(T.idn[:, :], T.idn1[:, :], [[-1, 128]], A.is_equal, 0.0, 0, 1), k_one)
     k_bc = ms(T.bc[:, :], -2.0 ** -110)
     k_p = ts(T.pi[:, 0:1], T.pc[:, :], 15, None, A.bitwise_and, deps=(g_pc,))
     k_p = ts(T.pi[:, 1:2], T.pc[:, :], 3, 1, A.logical_shift_right, A.bitwise_and)
-    k_p = ts(T.pi[:, 2:3], T.pc[:, :], 4, None, A.logical_shift_right)
-    k_uo = ts(T.uoj[:, :], T.uoi[:, :], 127, None, A.bitwise_and, deps=(g_uo,))
-    k_jr = ts(T.jr[:, :], T.ji[:, :], 15, None, A.bitwise_and, deps=(g_ji,))
-    k_pf = cp(T.pf[:, 0:3], T.pi[:, 0:3], k_p)
-    k_uu = cp(T.uou[:, :], T.uoj[:, :], k_uo)
-    k_f = ts(T.f1[:, 0:16], T.jr[:, :], 0.0, K, A.is_equal, A.mult, deps=(k_jr,))
-    k_f = ts(T.f1[:, 16:32], T.jr[:, :], 15.0, -2 * K, A.is_equal, A.mult)
+    k_uo = ts(T.uj[:, 0:16], T.ui[:, 0:16], 127, None, A.bitwise_and, deps=(g_uo,))
+    k_jr = ts(T.uj[:, 16:32], T.ui[:, 16:32], 15, None, A.bitwise_and, deps=(g_ji,))
+    k_pf = cp(T.pf[:, 0:2], T.pi[:, 0:2], k_p)
+    k_uu = cp(T.uou[:, :], T.uj[:, 0:16], k_uo)
+    k_f = ts(T.f1[:, 0:16], T.uj[:, 16:32], 0.0, K, A.is_equal, A.mult, deps=(k_jr,))
+    k_f = ts(T.f1[:, 16:32], T.uj[:, 16:32], 15.0, -2 * K, A.is_equal, A.mult)
     k_per = ts(T.per[:, :], T.jv[:, 0:L], 0.0, T.pf[:, 0:1], A.mult, A.add, deps=(g_jv, k_pf))
     k_f = tt(T.f3[:, :], T.f1[:, 0:16], T.f1[:, 16:32], A.add, k_f)
-    k_htn = cp(T.htn[:, :], T.htj[:, :], ("dn", 16))
+    c0 = ts(T.pf[:, 3:4], T.pf[:, 1:2], -1.0, 1.0, A.mult, A.add)
+    c0 = ts(T.pf[:, 6:7], T.pf[:, 0:1], 0.0, 2 * K, A.is_equal, A.mult)
+    sl = [ts(T.slot[:, 2 * L * i:2 * L * (i + 1)], T.jv[:, :], T.pf[:, 0:1], None, A.add) for i in range(2)]
+    f4 = cp(T.f4[:, :], T.f3[:, :], k_f)
+    iv = ms(T.iv[:, :], -K)
+    cw = ts(T.cw[:, 0:1], T.pf[:, 6:7], -K, None, A.add, deps=(c0,))
+    cw = ts(T.cw[:, 1:2], T.pf[:, 6:7], 1.0 - K, None, A.add)
+    cv = ts(T.cv[:, :], T.pf[:, 6:7], -K, None, A.add)
+    f4 = ms(T.f4[0:16, :], 0.0, f4)
+    iv = ts(T.iv[0:16, :], T.pf[0:16, 0:1], K - 16, None, A.add, deps=(iv,))
+    cv = ms(T.cv[0:16, :], -K, cv)
+    f4 = ms(T.f4[0:16, 0:1], 16.0, f4)
     k_fw = act(T.fw[:, :], T.f3[:, :].indirect(T.per[:, :]), k_f, k_per)
+    k_fv = act(T.fv[:, :], T.f4[:, :].indirect(T.per[:, :]), f4)
+    k_static = [k_fv, cv, iv, sl]
     k_u = qu(T.uq[:, :], T.us[:, :], T.ut[:, :], ("du", 16))
     k_up = cp(T.uqp[:, :].bitcast(dt.uint32), T.uq[:, :].bitcast(dt.uint32).indirect(T.uou[:, :]), k_u, k_uu)
     k_us = act(T.usp[:, :], T.us[:, :].indirect(T.uou[:, :]), k_u, k_uu)
-    need("gp", k_htn)
-    out_to([(c, T.htn[:, :], T.hr[:, :], "rh") for c, _, _, _ in host_tables(near, far)], 4)
 
-    def tables(k, *deps):
-        gt, d, e = T["gt%d" % k], T["dtab%d" % k], T["etab%d" % k]
-        t = [None]
-
-        def s0():
-            t[0] = cp(T.gf[:, :], gt[:, :], *deps)
-
-        def s1():
-            t[0] = tt(d[:, :], T.gf[:, 2 * L:4 * L], T.gf[:, 0:2 * L], A.subtract, t[0])
-
-        def s2():
-            t[0] = ts(T.kd[:, :], d[:, :], T.cw[:, 1:2], None, A.mult, deps=(t[0],))
-
-        def s3():
-            t[0] = tt(e[:, :], T.kd[:, :], T.gf[:, 0:2 * L], A.add, t[0])
-            tab[k] = t[0]
-        return [s0, s1, s2, s3]
+    def window(k, i):
+        win[k] = act(T.gw[:, C * i:C * i + C], T.ramp[:, :].indirect(T["gt%d" % k][:, L * i:L * i + L]), g_rm, tab[k])
 
     def guests(k):
-        return ("g%d" % k, len(share(topo, backs[k][1][1], core, 0, 2)))
+        tab[k] = cp(T["gt%d" % k][:, :], T["tab%d" % k][:, 0:2 * L], ("g%d" % k, len(share(topo, backs[k][1][1], core, 0, 2))))
 
-    def step(o, win, off, c, tok, h=LA):
-        r = []
-        if h:
-            r.append(cp(o[:, 0:16 * h], win[:, :].indirect(off[:, c:c + h]), tok))
-        r.append(act(o[:, 16 * h:C], win[:, :].indirect(off[:, c + h:c + L]), tok))
-        return r
+    def hosts(k):
+        n = sum(len(share(topo, c, core, 0, 1)) for c, kk, _, _ in host_tables(*backs[k]) if kk == k)
+        hq[k] = cp(T["hq%d" % k][:, :], T["hi%d" % k][:, :], ("h%d" % k, n))
 
-    xtok, ytok, psfree, tab = [[("dx0", 16)], [("dx1", 16)]], None, [], {}
+    xtok, ytok, psfree, addread, tab, win, hq = [[("dx0", 16)], [("dx1", 16)]], [], [], [], {}, {}, {}
     for k in range(4):
         xt, xb, xq, xs = T["xt%d" % k], T["xb%d" % (k % 2)], T["xq%d" % k], T["xs%d" % k]
         q0 = []
@@ -276,139 +275,139 @@ def rank_program(g, core, T, topo):
                 out_to([((near[0], far[0])[i], u8(xq[:, a:e]), u8(T["ca%d" % k][:, 0:e - a]), "rc%d" % k)], 1)
         if k == 3:
             break
-        rc, rs, hq, vl = T["rc%d" % k], T["rs%d" % k], T["hq%d" % k], T["vl%d" % k]
+        rc, rs, vl, tb = T["rc%d" % k], T["rs%d" % k], T["vl%d" % k], T["tab%d" % k]
         zt, zq, zs, xn, yn = T["zt%d" % k], T["zq%d" % k], T["zs%d" % k], T["xt%d" % (k + 1)], T["xb%d" % ((k + 1) % 2)]
         back = backs[k]
         out_to([(far[1], xs[:, :], T["sa%d" % k][:, :], "rc%d" % k)], 1)
         if k == 0:
-            g_id = op("gp", lambda: g.affine_select(T.idn[:, :], T.idn1[:, :], [[-1, 128]], A.is_equal, 0.0, 0, 1), k_one)
-            g_rm = iota(T.ramp[:, :], [[1, C]], 0, 0, True)
             k_hto = cp(T.hto[:, :], T.hti[:, :], ("dh", 64))
         sa, sb = [], []
         for i, (a, e) in enumerate(PARTS):
             m = [mm(bank(4 * i + d, e - a), T.uqp[:, 128 * d:128 * d + 128], T.usp[:, 128 * d:128 * d + 128], xq[:, a:e], xs[:, a:e], q0[i], k_up, k_us, psfree) for d in range(2)]
-            sa.append(ts(T.sg[:, a:e], bank(4 * i, e - a), 0.0, 0.5, A.is_gt, A.subtract, deps=(m[0],)))
+            sa.append(ts(T.sg[:, a:e], bank(4 * i, e - a), 0.0, float(C), A.is_gt, A.mult, deps=(m[0],)))
             need("se", m[1], k_bc)
             sb.append(op("se", lambda i=i, a=a, e=e: s.activation(T.sg[:, C + a:C + e], bank(4 * i + 1, e - a), AF.Sign, bias=T.bc[:, 0:1])))
-        ga = cp(T.gm[:, 0:C], T.sg[:, 0:C].indirect(T.hto[:, 0:L]), sa, k_hto)
-        gb = act(T.gm[:, C:2 * C], T.sg[:, C:2 * C].indirect(T.hto[:, L:2 * L]), sb, k_hto, scale=0.5)
-        sc = [lay(T.sc[:, C * d:C * d + C], T.gm[:, C * d:C * d + C], T.fw[:, :], -K, (ga, gb)[d], k_fw) for d in range(2)]
+        ga = tt(T.ga[:, :], T.sg[:, 0:C].indirect(T.hto[:, 0:L]), T.ramp[:, :], A.add, sa, k_hto, g_rm)
+        gb = act(T.gb[:, :], T.sg[:, C:2 * C].indirect(T.hto[:, L:2 * L]), sb, k_hto)
+        sca = lay(T.sc[:, 0:C], T.ga[:, :], T.fw[:, :], -K, ga, k_fw)
+        scb = lay(T.sc[:, C:2 * C], T.gb[:, :], T.fw[:, :], -K, gb) if k == 0 else None
+        ua = ts((T.ul if k else T.bl)[:, 0:L], T.sc[:, 15:C:16], T.cw[:, 0:1], None, A.add, deps=(sca, cw))
         psfree = psfree + sa + sb
         call = ("c%d" % k, sum(len(share(topo, c, core, 0, 1)) for c in (back[0][0], back[1][0], back[1][1])))
         msg = ("m%d" % k, len(share(topo, back[0][1], core, 0, 1)))
-        hs = ("h%d" % k, sum(len(share(topo, c, core, 0, 1)) for c, kk, _, _ in host_tables(*back) if kk == k))
-        dc, lg = [], []
+        dc, lg, plan = {}, {}, HOST if k else GUEST
 
         def unpack(b):
             i = (2, 3, 6, 7)[b]
             m = mm(bank(i, C), T.eq[:, 128 * b:128 * b + 128], T.es[:, 128 * b:128 * b + 128], rc[:, :], rs[:, :], call, k_eq, addread)
-            dc.append(act(T.ds[:, C * b:C * b + C], bank(i, C), m))
+            dc[b] = act(T.ds[:, C * b:C * b + C], bank(i, C), m)
 
         def larger(b):
-            lg.append(tt(T.mm[:, C * b:C * b + C], T.ds[:, C * b:C * b + C].indirect(hq[:, :]), xt[:, b:4 * C:4], A.max, dc[b], hs))
+            lg[b] = tt(T.mm[:, C * b:C * b + C], T.ds[:, C * b:C * b + C].indirect(T["hq%d" % k][:, :]), xt[:, b:4 * C:4], A.max, dc[b], hq[k])
+
+        def step(i, o, w, off, c, tok, between=None):
+            r, (h, copies, picks) = [], plan[i]
+            if h:
+                r.append(cp(o[:, 0:16 * h], w[:, :].indirect(off[:, c:c + h]), tok))
+            r.append(act(o[:, 16 * h:C], w[:, :].indirect(off[:, c + h:c + L]), tok))
+            r2 = between() if between else None
+            for b in picks:
+                larger(b)
+            for b in copies:
+                unpack(b)
+            return r, r2
 
         def lists(src, *deps):
-            n = tt(T.nt[:, :], src, T["dtab%d" % k][:, :], A.mult, tab[k], *deps)
-            n = tt(T.nf[:, :], T.nt[:, :], T["etab%d" % k][:, :], A.add, n)
-            return cp(T.nu[:, :], T.nf[:, :], n)
+            n = tt(T.nt[:, 0:L], src, tb[:, 2 * L:3 * L], A.mult, tab[k], *deps)
+            n = tt(T.nt[:, L:2 * L], T.nt[:, 0:L], tb[:, 3 * L:4 * L], A.add, n)
+            return cp(T.nu[:, :], T.nt[:, L:2 * L], n)
 
-        def rest(t2):
+        def walk(ul, tok, signs):
+            t, n = step(0, T.ya, T.gw, ul, 0, [tok, win[k]], signs)
+            t2, _ = step(1, T.yb, T.ya, T.nu, 0, [t, n])
             c = lay(T.sp[:, :], T.yb[:, :], T.fv[:, :], T.iv[:, 0:1], t2, k_static)
 
             def on(e, a, w):
                 return ts(T.slot[a + 32 * e:a + 32 * e + w, L * e:L * e + L], T.sp[a:a + w, 15:C:16], T.cv[a:a + w, 0:1], None, A.add, deps=(c,))
             c1 = [on(1, a, 32) for a in (0, 32, 64)]
-            t = step(T.ya, T.yb, T.slot, L, [t2, c1])
-            c2 = on(2, 0, 64)
-            c3 = on(3, 0, 32)
-            t = step(T.yb, T.ya, T.slot, 2 * L, [t, c2])
-            t = step(T.ya, T.yb, T.slot, 3 * L, [t, c3])
+            t, c2 = step(2, T.ya, T.yb, T.slot, L, [t2, c1], lambda: [on(2, 0, 64), on(3, 0, 32)])
+            t, _ = step(3, T.yb, T.ya, T.slot, 2 * L, [t, c2])
+            t, _ = step(4, T.ya, T.yb, T.slot, 3 * L, [t])
+            if k == 0:
+                guests(1)
+                window(1, 1)
             c = lay(T.sv[:, :], T.ya[:, :], T.fv[:, :], T.iv[:, 0:1], t)
             return t, ts(vl[:, :], T.sv[:, 15:C:16], T.cv[:, 0:1], None, A.add, deps=(c,))
 
         if k == 0:
-            k_bl = cp(T.bl[:, :], T.sc[:, 15:2 * C:16], sc)
-            need("gp", k_bl)
+            ub = ts(T.bl[:, L:2 * L], T.sc[:, C + 15:2 * C:16], T.cw[:, 1:2], None, A.add, deps=(scb,))
+            need("gp", ua, ub)
             out_to([(near[1], T.bl[:, :], T.br[:, :], "rm0")], 1)
             ytok = [act(xb[:, :], xt[:, :], xtok, scale=64.0)]
-            ec = [cp(T.et[:, 512 * b + b:512 * b + 512:4], T.idn[:, :], k_et, g_id) for b in range(4)]
-            c0 = ts(T.pf[:, 3:4], T.pf[:, 1:2], -1.0, 1.0, A.mult, A.add, deps=(k_pf,))
-            c0 = ts(T.pf[:, 4:5], T.pf[:, 2:3], 1.0, None, A.not_equal)
-            c0 = ts(T.pf[:, 5:6], T.pf[:, 2:3], 1.0, None, A.is_equal)
-            c0 = ts(T.pf[:, 6:7], T.pf[:, 0:1], 0.0, 2 * K, A.is_equal, A.mult)
-            jp = ts(T.jp[:, :], T.jv[:, :], T.pf[:, 0:1], None, A.add)
-            k_eq = qu(T.eq[:, :], T.es[:, :], T.et[:, :], ec)
-            e1 = ts(T.t1[:, :], T.eo[:, 0:8 * L:2], T.pf[:, 3:4], None, A.mult, deps=(("de", 32), c0))
-            e2 = ts(T.t2[:, :], T.eo[:, 1:8 * L:2], T.pf[:, 1:2], None, A.mult)
-            jm = ts(T.jm[:, :], T.jp[:, :], T.pf[:, 5:6], None, A.mult, deps=(jp,))
-            cw = ts(T.cw[:, 0:1], T.pf[:, 6:7], -K, None, A.add)
-            cv = ts(T.cv[:, :], T.pf[:, 6:7], -K, None, A.add)
-            ck = ts(T.cw[:, 1:2], T.pf[:, 6:7], 0.5 - K, None, A.add)
-            e3 = tt(T.sel[:, :], T.t1[:, :], T.t2[:, :], A.add, e1, e2)
-            f4 = cp(T.f4[:, :], T.f3[:, :])
-            iv = ms(T.iv[:, :], -K)
-            sl = [cp(T.slot[:, 2 * L * i:2 * L * (i + 1)], T.jp[:, :]) for i in range(2)]
-            e4 = ts(T.selb[:, :], T.sel[:, 2 * L:4 * L], T.pf[:, 4:5], None, A.mult, deps=(e3,))
-            f4 = ms(T.f4[0:16, :], 0.0, f4)
-            cv = ms(T.cv[0:16, :], -K, cv)
-            iv = ts(T.iv[0:16, :], T.pf[0:16, 0:1], K - 16, None, A.add, deps=(iv,))
-            e5 = tt(T.selc[:, :], T.selb[:, :], T.jm[:, :], A.add, e4, jm)
-            f4 = ms(T.f4[0:16, 0:1], 16.0, f4)
-            e6 = [cp(T.gt0[:, 2 * L * i:2 * L * i + L], T.sel[:, L * i:L * i + L]) for i in range(2)]
-            e6 += [cp(T.gt0[:, 2 * L * i + L:2 * L * (i + 1)], T.selc[:, L * i:L * i + L], e5) for i in range(2)]
-            k_fv = act(T.fv[:, :], T.f4[:, :].indirect(T.per[:, :]), f4)
-            k_static = [k_fv, cw, cv, iv, sl]
-            need("gp", e6)
-            out_to([(far[1], T.gt0[:, :], T.gr[:, :], "rg")], 1)
-            for f in tables(0, e6, ck):
-                f()
+            e1 = ts(T.t1[:, 0:4 * L], T.eo[:, 0:8 * L:2], T.pf[:, 3:4], None, A.mult, deps=(("de", 48), g_eo, c0))
+            e2 = ts(T.t1[:, 4 * L:8 * L], T.eo[:, 1:8 * L:2], T.pf[:, 1:2], None, A.mult)
+            k_ec = cp(T.et[:, 4:516:4], T.idn[:, :], k_et, g_id)
+            e3 = tt(tb[:, 0:2 * L], T.t1[:, 0:2 * L], T.t1[:, 4 * L:6 * L], A.add, e1, e2)
+            e4 = tt(T.sel[:, 0:2 * L], T.t1[:, 2 * L:4 * L], T.t1[:, 6 * L:8 * L], A.add)
+            tab[0] = cp(T.gt0[:, :], tb[:, 0:2 * L], e3)
+            for i in range(2):
+                window(0, i)
+
+            def unit(b):
+                return qu(T.eq[:, 128 * b:128 * b + 128], T.es[:, 128 * b:128 * b + 128], T.et[:, 4 - b:516 - b], k_ec)
+            e5 = tt(T.sel[:, 2 * L:3 * L], T.sel[:, L:2 * L], T.sel[:, 0:L], A.subtract, e4)
+            unit(0)
+            ts(tb[:, 2 * L:3 * L], T.sel[:, 2 * L:3 * L], 0.5, None, A.mult, deps=(e5,))
+            e6 = ts(T.sel[:, 3 * L:4 * L], T.sel[:, 2 * L:3 * L], T.cw[:, 1:2], 0.5, A.mult, A.mult)
+            unit(1)
+            tab[0] = tt(tb[:, 3 * L:4 * L], T.sel[:, 3 * L:4 * L], T.sel[:, 0:L], A.add, e6)
+            need("gp", tab[0])
+            out_to([(far[1], tb[:, :], T.gr[:, :], "rg")], 1)
+            unit(2)
+            k_eq = unit(3)
+            hosts(0)
             need("sy", call)
             g.sync.dma_start(u8(T.wq[:, :]), T.wc[:, :]).then_inc(T.sem.dw, 16)
             g.sync.dma_start(T.wsc[:, :], T.ws[:, :]).then_inc(T.sem.dw, 16)
             g.sync.dma_start(T.vt[:, :], T.v[:, :]).then_inc(T.sem.dv, 16)
-            addread = []
-            for b in range(4):
-                unpack(b)
-            larger(0)
-            larger(1)
-            n = lists(T.bb[:, :], msg)
-            t = step(T.ya, T.ramp, T.nu, 0, [n, g_rm], 0)
-            larger(2)
-            t = step(T.yb, T.ya, T.nu, L, [t], 0)
-            larger(3)
-            t, k_vl = rest(t)
+
+            def signs():
+                return lists(T.nt[:, 2 * L:3 * L], ts(T.nt[:, 2 * L:3 * L], T.bb[:, L:2 * L], T.cw[:, 1:2], None, A.subtract, deps=(msg,)))
+            t, k_vl = walk(T.bb, msg, signs)
             mine = vl
         else:
-            n = lists(T.sc[:, 15:2 * C:16], sc)
-            t = step(T.ya, T.ramp, T.nu, 0, [n])
-            t = step(T.yb, T.ya, T.nu, L, [t])
-            t, c = rest(t)
+            def signs():
+                return lists(T.sc[:, C + 15:2 * C:16], lay(T.sc[:, C:2 * C], T.gb[:, :], T.fw[:, :], -K, gb))
+            t, c = walk(T.ul, ua, signs)
             need("gp", c)
             out_to([(near[1], vl[:, :], T["vr%d" % k][:, :], "rm%d" % k)], 1)
-            for b in range(4):
-                unpack(b)
             if k == 2:
                 c6 = cp(T.slot[0:16, 0:L], vl[96:112, :], c)
-                c7 = cp(T.l2[:, :], vl[:, :])
-            for b in range(4):
-                larger(b)
-            if k == 1:
-                for f in tables(2, guests(2)):
-                    f()
-            else:
                 t8 = act(T.yb[:, :], T.ya[:, :].indirect(T.slot[:, 0:L]), t, c6)
-                c8 = lay(T.sp[:, :], T.yb[:, :], T.fw[:, :], -K, t8)
-                c9 = ts(T.l2[0:16, :], T.sp[0:16, 15:C:16], T.cw[0:16, 0:1], None, A.add, deps=(c8, c7))
-                need("gp", c9)
-                out_to([(far[1], T.l2[:, :], T.pr[:, :], "rl")], 1)
+                need("sy", t)
+                g.sync.dma_start(T.po[0:112, :], T.ya[16:128:16, :]).then_inc(T.sem.dp, 16)
+                need("sy", t8)
+                g.sync.dma_start(T.po[112:128, :], T.yb[0:1, :]).then_inc(T.sem.dp, 16)
+                need("gp", ("dp", 32))
+                out_to([(far[1], T.po[:, :], T.pr[:, :], "rl")], 1)
             k_vl, mine = msg, T["rv%d" % k]
-        psfree = psfree + dc
+        for b in range(4):
+            if b not in dc:
+                unpack(b)
+        for b in range(4):
+            if b not in lg:
+                larger(b)
+        if k == 1:
+            for i in range(2):
+                window(2, i)
+        lg = list(lg.values())
+        psfree = psfree + list(dc.values())
         zc = [[], []]
 
         def mosaic(i, b, e):
             a, z = PARTS[i]
             o, w = zt[:, 4 * a + b:4 * z:4], T.mm[:, C * b:C * b + C].indirect(mine[:, a // 16:z // 16])
-            zc[i].append(cp(o, w, k_vl, lg) if e == "ve" else act(o, w, k_vl, lg))
+            zc[i].append(cp(o, w, k_vl, lg[b]) if e == "ve" else act(o, w, k_vl, lg[b]))
 
         xtok, ynew = [[], []], []
 
@@ -422,11 +421,10 @@ def rank_program(g, core, T, topo):
             ad = tt(yn[:, 4 * a + b:4 * z:4], bank(4 * i + b, z - a), xb[:, 4 * a + b:4 * z:4], A.add, m, ytok)
             xtok[i].append(act(xn[:, 4 * a + b:4 * z:4], yn[:, 4 * a + b:4 * z:4], ad, scale=2.0 ** -6))
             ynew.append(ad)
-        for i, b, e in ((0, 0, "ve"), (0, 2, "se"), (0, 1, "ve"), (0, 3, "se"), (1, 2, "se"), (1, 3, "se"), (1, 1, "se")):
+        for i, b, e in ((0, 2, "ve"), (0, 0, "se"), (0, 3, "ve"), (0, 1, "se"), (1, 0, "se"), (1, 1, "se"), (1, 2, "se")):
             mosaic(i, b, e)
         ma = layer(0)
-        mosaic(1, 0, "ve")
-        extra = tables(1, guests(1)) if k == 0 else []
+        mosaic(1, 3, "ve")
         for b in range(2):
             state(0, b, ma[b])
         mb = layer(1)
@@ -434,10 +432,13 @@ def rank_program(g, core, T, topo):
             state(0, b, ma[b])
         for b in range(4):
             state(1, b, mb[b])
-            if extra:
-                extra[b]()
         ytok = addread = ynew
         psfree = psfree + ynew
+        if k == 0:
+            window(1, 0)
+            hosts(1)
+            guests(2)
+            hosts(2)
         if k == 1:
             k_v = qu(T.vq[:, :], T.vs[:, :], T.vt[:, :], ("dv", 16))
 
@@ -451,15 +452,13 @@ def rank_program(g, core, T, topo):
     for i, (a, e) in enumerate(PARTS):
         m = mm(bank(4 * i, e - a), T.vq[:, :], T.vs[:, :], T.xq3[:, a:e], T.xs3[:, a:e], q0[i], k_v, psfree)
         yc.append(cp(T.yt[:, a:e], bank(4 * i, e - a), m))
-    pltok = act(T.plr[:, :], T.ramp[:, :].indirect(T.rp[:, :]), ("pl", len(share(topo, backs[2][1][1], core, 0, 1))))
     for i, (a, e) in enumerate(PARTS):
         store("sy", T.oc[:, 4 * a:4 * e], u8(T.xq3[:, a:e]), q0[i])
     for b in range(4):
-        store("sy", T.osc[4 * b:4 * b + 4, :], T.xs3[32 * b:32 * b + 4, :])
-    store("se", T.pl[0:7, :], T.plr[16:128:16, :], pltok)
-    store("se", T.pl[7:8, :], T.plr[0:1, :])
+        store(("sy", "se")[b % 2], T.osc[4 * b:4 * b + 4, :], T.xs3[32 * b:32 * b + 4, :], q0)
     for i, (a, e) in enumerate(PARTS):
         store(("se", "sy")[i], T.y[:, a:e], T.yt[:, a:e], yc[i])
+    store("se", T.pl[:, :], T.pn[:, :], ("pl", len(share(topo, backs[2][1][1], core, 0, 1))))
     g.sync.wait_ge(T.sem.do, do[0])
     for e in ("ve", "se", "pe", "gp"):
         need("gp", (e, count[e]))

from concourse.bass import DstId, RemoteDMATransfer
from concourse.mybir import dt, AluOpType, ActivationFunctionType

C = 352
STEP = [1, 2, 4]
L = C // 16
LA = 12
LW = 12
F8 = "float8_e4m3fn_x4"
K = 1024.0
BANK = 512
GUEST = [(0, (0,), ()), (0, (1, 2), (0,)), (0, (3,), (1,)), (0, (), (2, 3)), (LW, (), ())]
HOST = [(0, (), ()), (LW, (), ()), (LW, (), ()), (LW, (), ()), (LW, (0, 1, 2, 3), ())]

SCRATCH = {
    "ut": ("sbuf", [128, 512], "bfloat16"), "uq": ("sbuf", [128, 128], F8), "us": ("sbuf", [128, 128], "uint8"),
    "uqp": ("sbuf", [128, 256], F8), "usp": ("sbuf", [128, 256], "uint8"),
    "vt": ("sbuf", [128, 512], "bfloat16"), "vq": ("sbuf", [128, 128], F8), "vs": ("sbuf", [128, 128], "uint8"),
    "wq": ("sbuf", [128, 512], F8), "wsc": ("sbuf", [128, 512], "uint8"),
    "idn1": ("sbuf", [128, 128], "float32"), "idn": ("sbuf", [128, 128], "float32"),
    "et": ("sbuf", [128, 516], "bfloat16"), "eq": ("sbuf", [128, 512], F8), "es": ("sbuf", [128, 512], "uint8"),
    "hti": ("sbuf", [128, 2 * L], "int32"), "htj": ("sbuf", [128, L], "int32"), "hto": ("sbuf", [128, 2 * L], "uint16"),
    "gd": ("dram", [10, 64 * L], "int32"), "eo": ("sbuf", [128, 8 * L], "int32"),
    "pc": ("sbuf", [128, 1], "int32"), "pi": ("sbuf", [128, 8], "int32"), "pf": ("sbuf", [128, 8], "float32"),
    "bc": ("sbuf", [128, 1], "float32"), "cw": ("sbuf", [128, 4], "float32"), "cv": ("sbuf", [128, 1], "float32"),
    "iv": ("sbuf", [128, 1], "float32"), "xb0": ("sbuf", [128, 4 * C], "bfloat16"), "xb1": ("sbuf", [128, 4 * C], "bfloat16"),
    "ui": ("sbuf", [128, 32], "int32"), "uj": ("sbuf", [128, 32], "int32"), "uou": ("sbuf", [128, 16], "uint16"),
    "f1": ("sbuf", [128, 32], "float32"), "f3": ("sbuf", [128, 16], "float32"), "f4": ("sbuf", [128, 16], "float32"),
    "ramp": ("sbuf", [128, C], "float32"), "jv": ("sbuf", [128, 2 * L], "float32"), "per": ("sbuf", [128, L], "uint16"),
    "fw": ("sbuf", [128, C], "bfloat16"), "fv": ("sbuf", [128, C], "bfloat16"),
    "t1": ("sbuf", [128, 8 * L], "float32"), "sel": ("sbuf", [128, 4 * L], "float32"), "gw": ("sbuf", [128, 2 * C], "float32"),
    "sg": ("sbuf", [128, 2 * C], "bfloat16"), "ga": ("sbuf", [128, C], "float16"), "gb": ("sbuf", [128, C], "bfloat16"),
    "sc": ("sbuf", [128, 2 * C], "float16"), "bl": ("sbuf", [128, 2 * L], "uint16"), "bb": ("sbuf", [128, 2 * L], "uint16"),
    "nt": ("sbuf", [128, 4 * L], "float32"), "nu": ("sbuf", [128, L], "uint16"), "ul": ("sbuf", [128, L], "uint16"),
    "ya": ("sbuf", [128, C], "float32"), "yb": ("sbuf", [128, C], "float32"),
    "sp": ("sbuf", [128, C], "float32"), "sv": ("sbuf", [128, C], "float32"), "slot": ("sbuf", [128, 4 * L], "uint16"),
    "po": ("dram", [128, L], "float32"), "pn": ("dram", [128, L], "float32"),
    "ds": ("sbuf", [128, 4 * C], "bfloat16"), "mm": ("sbuf", [128, 4 * C], "bfloat16"), "yt": ("sbuf", [128, C], "float32"),
    "ps": ("psum", [128, 8 * BANK], "float32"),
    "hr": ("sbuf", [128, L], "int32"), "gr": ("sbuf", [128, 4 * L], "float32"), "br": ("sbuf", [128, 2 * L], "uint16"), "pr": ("dram", [128, L], "float32"),
}
for _k in range(4):
    SCRATCH["xt%d" % _k] = ("sbuf", [128, 4 * C], "bfloat16")
    SCRATCH["xq%d" % _k] = ("sbuf", [128, C], F8)
    SCRATCH["xs%d" % _k] = ("sbuf", [128, C], "uint8")
for _k in range(3):
    SCRATCH["rc%d" % _k] = ("sbuf", [128, C], F8)
    SCRATCH["rs%d" % _k] = ("sbuf", [128, C], "uint8")
    SCRATCH["zt%d" % _k] = ("sbuf", [128, 4 * C], "bfloat16")
    SCRATCH["zq%d" % _k] = ("sbuf", [128, C], F8)
    SCRATCH["zs%d" % _k] = ("sbuf", [128, C], "uint8")
    SCRATCH["vl%d" % _k] = ("sbuf", [128, L], "uint16")
    SCRATCH["hi%d" % _k] = ("sbuf", [128, L], "int32")
    SCRATCH["hq%d" % _k] = ("sbuf", [128, L], "uint16")
    SCRATCH["tab%d" % _k] = ("sbuf", [128, 4 * L], "float32")
    SCRATCH["gt%d" % _k] = ("sbuf", [128, 2 * L], "uint16")
    SCRATCH["ca%d" % _k] = ("sbuf", [128, C - 128], F8)
    SCRATCH["sa%d" % _k] = ("sbuf", [128, C], "uint8")
for _k in (1, 2):
    SCRATCH["vr%d" % _k] = ("sbuf", [128, L], "uint16")
    SCRATCH["rv%d" % _k] = ("sbuf", [128, L], "uint16")

SEMAPHORES = ["ve", "se", "pe", "gp", "dx0", "dx1", "du", "dn", "dh", "dg", "dw", "dv", "de", "dp", "do", "sent", "rh", "rg", "rl", "pl"]
for _k in range(3):
    SEMAPHORES += ["c%d" % _k, "m%d" % _k, "h%d" % _k, "g%d" % _k, "rc%d" % _k, "rm%d" % _k]


def parts():
    return [(0, 16 * LA), (16 * LA, C)]


def share(topo, src, dst, i, n):
    return topo.engines(src, dst)[i::n]


def send(g, core, T, topo, moves, n):
    ts, total = [], 0
    for i, (dst, a, b, sem) in enumerate(moves):
        e = share(topo, core, dst, i, n)
        rid, pid = topo.addr(dst, core)
        ts.append(RemoteDMATransfer(dst_ids=[DstId(rid=rid, pnc=pid)], dma_engine_mask=sum(1 << j for j in e), remote_sem=T.sem[sem], srcs=[a], dsts=[b]))
        total += len(e)
    g.remote_dma_fused(ts, local_sem=T.sem.sent)
    return total


def handers(topo, core, partner):
    r = [c for c in topo.cores_of(core) if c != core and topo.may_write(c, partner)]
    return [c for c in r if topo.die(c) == topo.die(core)], [c for c in r if topo.die(c) != topo.die(core)]


def host_tables(near, far):
    return [(near[1], 0, 0, L), (near[0], 1, 0, L), (far[0], 2, 0, L // 2), (far[1], 2, L // 2, L)]


def u8(v):
    return v.bitcast(dt.uint8)


def hand_on(g, core, T, topo, home, near, far):
    rank = T.rank_of(home)
    mates = [T.cores[rank ^ s] for s in STEP]
    sent, whole = 0, len(share(topo, home, core, 0, 1))
    for i, (c, k, a, e) in enumerate(host_tables(near, far)):
        if c == core:
            g.wait_ge(T.sem.rh, len(share(topo, home, core, i, 4)))
            sent += send(g, core, T, topo, [(mates[k], T.hr[:, a:e], T["hi%d" % k][:, a:e], "h%d" % k)], 1)
    for k in range(3):
        if core in (near[0], far[0]):
            a, e = parts()[0 if core == near[0] else 1]
            g.wait_ge(T.sem["rc%d" % k], whole)
            sent += send(g, core, T, topo, [(mates[k], u8(T["ca%d" % k][:, 0:e - a]), u8(T["rc%d" % k][:, a:e]), "c%d" % k)], 1)
        elif core == near[1]:
            g.wait_ge(T.sem["rm%d" % k], whole)
            a, b = (T["vr%d" % k], T["rv%d" % k]) if k else (T.br, T.bb)
            sent += send(g, core, T, topo, [(mates[k], a[:, :], b[:, :], "m%d" % k)], 1)
        else:
            g.wait_ge(T.sem["rc%d" % k], whole)
            sent += send(g, core, T, topo, [(mates[k], T["sa%d" % k][:, :], T["rs%d" % k][:, :], "c%d" % k)], 1)
            if k == 0:
                g.wait_ge(T.sem.rg, whole)
                sent += send(g, core, T, topo, [(mates[j], T.gr[:, :], T["tab%d" % j][:, :], "g%d" % j) for j in (1, 2)], 2)
            if k == 2:
                g.wait_ge(T.sem.rl, whole)
                sent += send(g, core, T, topo, [(mates[k], T.pr[:, :], T.pn[:, :], "pl")], 1)
    g.wait_ge(T.sem.sent, sent)


def rank_program(g, core, T, topo):
    rank = T.rank_of(core)
    if rank is None:
        for home in T.cores:
            if core in topo.cores_of(home):
                near, far = handers(topo, home, T.cores[T.rank_of(home) ^ STEP[0]])
                if core in near[:2] + far[:2]:
                    hand_on(g, core, T, topo, home, near, far)
        return
    A, AF, PARTS = AluOpType, ActivationFunctionType, parts()
    mates = [T.cores[rank ^ s] for s in STEP]
    near, far = handers(topo, core, mates[0])
    backs = [handers(topo, m, core) for m in mates]
    queue = {"ve": g.vector, "se": g.scalar, "pe": g.tensor, "gp": g, "sy": g.sync}
    count, seen, sent = {"ve": 0, "se": 0, "pe": 0, "gp": 0}, {}, [0]

    def need(e, *toks):
        for t in toks:
            if isinstance(t, list):
                need(e, *t)
            elif t is not None and seen.get((e, t[0]), 0) < t[1]:
                queue[e].wait_ge(T.sem[t[0]], t[1])
                seen[(e, t[0])] = t[1]

    def op(e, call, *deps):
        need(e, *deps)
        count[e] += 1
        call().then_inc(T.sem[e], 1)
        return (e, count[e])

    v, s, p = g.vector, g.scalar, g.tensor

    def ts(out, in0, s1, s2, o0, o1=None, deps=()):
        if o1 is None:
            return op("ve", lambda: v.tensor_scalar(out, in0, s1, None, o0), *deps)
        return op("ve", lambda: v.tensor_scalar(out, in0, s1, s2, o0, o1), *deps)

    def tt(out, a, b, o, *deps):
        return op("ve", lambda: v.tensor_tensor(out, a, b, o), *deps)

    def cp(out, a, *deps):
        return op("ve", lambda: v.tensor_copy(out, a), *deps)

    def ms(ap, c, *deps):
        return op("ve", lambda: v.memset(ap, c), *deps)

    def qu(q, qs, t, *deps):
        return op("ve", lambda: v.quantize_mx(q, qs, t), *deps)

    def lay(out, a, f, first, *deps):
        return op("ve", lambda: v.tensor_tensor_scan(out, a, f, first, A.max, A.add), *deps)

    def act(out, a, *deps, scale=1.0):
        if scale == 1.0:
            return op("se", lambda: s.activation(out, a, AF.Copy), *deps)
        return op("se", lambda: s.activation(out, a, AF.Copy, scale=scale), *deps)

    def mm(out, q, qs, x, xs, *deps):
        return op("pe", lambda: p.matmul_mx(out, q, qs, x, xs, True, True), *deps)

    def out_to(moves, n):
        sent[0] += send(g, core, T, topo, moves, n)

    def bank(i, n):
        return T.ps[:, BANK * i:BANK * i + n]

    def iota(ap, pat, base, cm, f=False):
        if f:
            return op("gp", lambda: g.iota(ap, pat, base, cm, allow_small_or_imprecise_dtypes=True))
        return op("gp", lambda: g.iota(ap, pat, base, cm))

    g.sync.dma_start(T.htj[:, :], T.ht[:, :]).then_inc(T.sem.dn, 16)
    g.sync.dma_start(T.ut[:, :], T.u[:, :]).then_inc(T.sem.du, 16)
    for i, (a, e) in enumerate(PARTS):
        g.sync.dma_start(T.xt0[:, 4 * a:4 * e], T.x[:, 4 * a:4 * e]).then_inc(T.sem["dx%d" % i], 16)
    for d in range(2):
        w = 16 * (d + 1)
        g.sync.dma_start(T.hti[w:128, L * d:L * d + L], T.ht[0:128 - w, :]).then_inc(T.sem.dh, 16)
        g.sync.dma_start(T.hti[0:w, L * d:L * d + L], T.ht[128 - w:128, :]).then_inc(T.sem.dh, 16)
    for h in range(2):
        g.scalar.dma_start(T.gd[2:10, 32 * L * h:32 * L * (h + 1)], T.gl[:, :]).then_inc(T.sem.dg, 16)
        g.scalar.dma_start(T.gd[0:2, 32 * L * h:32 * L * (h + 1)], T.gl[96:128, :]).then_inc(T.sem.dg, 16)

    k_one = ms(T.idn1[:, :], 1.0)
    k_et = ms(T.et[:, :], 0.0)
    g_pc = iota(T.pc[:, :], [[1, 1]], 0, 1)
    g_uo = iota(T.ui[:, 0:16], [[-16, 2], [16, 8]], 112, 0)
    g_ji = iota(T.ui[:, 16:32], [[1, 16]], 128, -1)
    g_jv = iota(T.jv[:, :], [[0, 2], [16, L]], 0, 0, True)
    g_eo = iota(T.eo[:, 4 * L:8 * L], [[0, 2], [16, L], [0, 2]], -16, 1)
    g_rm = iota(T.ramp[:, :], [[1, C]], 0, 0, True)
    need("sy", ("dg", 64), g_eo)
    g.sync.dma_start(T.eo[:, 0:4 * L], T.gd[1:9, :]).then_inc(T.sem.de, 16)
    g.sync.dma_start(T.eo[0:16, 4 * L:8 * L], T.gd[0:1, :]).then_inc(T.sem.de, 16)
    g.sync.dma_start(T.eo[32:128, 4 * L:8 * L], T.gd[2:8, :]).then_inc(T.sem.de, 16)
    need("gp", ("dn", 16))
    out_to([(c, T.htj[:, :], T.hr[:, :], "rh") for c, _, _, _ in host_tables(near, far)], 4)
    g_id = op("gp", lambda: g.affine_select(T.idn[:, :], T.idn1[:, :], [[-1, 128]], A.is_equal, 0.0, 0, 1), k_one)
    k_bc = ms(T.bc[:, :], -2.0 ** -110)
    k_p = ts(T.pi[:, 0:1], T.pc[:, :], 15, None, A.bitwise_and, deps=(g_pc,))
    k_p = ts(T.pi[:, 1:2], T.pc[:, :], 3, 1, A.logical_shift_right, A.bitwise_and)
    k_uo = ts(T.uj[:, 0:16], T.ui[:, 0:16], 127, None, A.bitwise_and, deps=(g_uo,))
    k_jr = ts(T.uj[:, 16:32], T.ui[:, 16:32], 15, None, A.bitwise_and, deps=(g_ji,))
    k_pf = cp(T.pf[:, 0:2], T.pi[:, 0:2], k_p)
    k_uu = cp(T.uou[:, :], T.uj[:, 0:16], k_uo)
    k_f = ts(T.f1[:, 0:16], T.uj[:, 16:32], 0.0, K, A.is_equal, A.mult, deps=(k_jr,))
    k_f = ts(T.f1[:, 16:32], T.uj[:, 16:32], 15.0, -2 * K, A.is_equal, A.mult)
    k_per = ts(T.per[:, :], T.jv[:, 0:L], 0.0, T.pf[:, 0:1], A.mult, A.add, deps=(g_jv, k_pf))
    k_f = tt(T.f3[:, :], T.f1[:, 0:16], T.f1[:, 16:32], A.add, k_f)
    c0 = ts(T.pf[:, 3:4], T.pf[:, 1:2], -1.0, 1.0, A.mult, A.add)
    c0 = ts(T.pf[:, 6:7], T.pf[:, 0:1], 0.0, 2 * K, A.is_equal, A.mult)
    sl = [ts(T.slot[:, 2 * L * i:2 * L * (i + 1)], T.jv[:, :], T.pf[:, 0:1], None, A.add) for i in range(2)]
    f4 = cp(T.f4[:, :], T.f3[:, :], k_f)
    iv = ms(T.iv[:, :], -K)
    cw = ts(T.cw[:, 0:1], T.pf[:, 6:7], -K, None, A.add, deps=(c0,))
    cw = ts(T.cw[:, 1:2], T.pf[:, 6:7], 1.0 - K, None, A.add)
    cv = ts(T.cv[:, :], T.pf[:, 6:7], -K, None, A.add)
    f4 = ms(T.f4[0:16, :], 0.0, f4)
    iv = ts(T.iv[0:16, :], T.pf[0:16, 0:1], K - 16, None, A.add, deps=(iv,))
    cv = ms(T.cv[0:16, :], -K, cv)
    f4 = ms(T.f4[0:16, 0:1], 16.0, f4)
    k_fw = act(T.fw[:, :], T.f3[:, :].indirect(T.per[:, :]), k_f, k_per)
    k_fv = act(T.fv[:, :], T.f4[:, :].indirect(T.per[:, :]), f4)
    k_static = [k_fv, cv, iv, sl]
    k_u = qu(T.uq[:, :], T.us[:, :], T.ut[:, :], ("du", 16))
    k_up = cp(T.uqp[:, :].bitcast(dt.uint32), T.uq[:, :].bitcast(dt.uint32).indirect(T.uou[:, :]), k_u, k_uu)
    k_us = act(T.usp[:, :], T.us[:, :].indirect(T.uou[:, :]), k_u, k_uu)

    def window(k, i):
        win[k] = act(T.gw[:, C * i:C * i + C], T.ramp[:, :].indirect(T["gt%d" % k][:, L * i:L * i + L]), g_rm, tab[k])

    def guests(k):
        tab[k] = cp(T["gt%d" % k][:, :], T["tab%d" % k][:, 0:2 * L], ("g%d" % k, len(share(topo, backs[k][1][1], core, 0, 2))))

    def hosts(k):
        n = sum(len(share(topo, c, core, 0, 1)) for c, kk, _, _ in host_tables(*backs[k]) if kk == k)
        hq[k] = cp(T["hq%d" % k][:, :], T["hi%d" % k][:, :], ("h%d" % k, n))

    xtok, ytok, psfree, addread, tab, win, hq = [[("dx0", 16)], [("dx1", 16)]], [], [], [], {}, {}, {}
    for k in range(4):
        xt, xb, xq, xs = T["xt%d" % k], T["xb%d" % (k % 2)], T["xq%d" % k], T["xs%d" % k]
        q0 = []
        for i, (a, e) in enumerate(PARTS):
            q0.append(qu(xq[:, a:e], xs[:, a:e], xt[:, 4 * a:4 * e], xtok[i]))
            if k < 3:
                need("gp", q0[i])
                out_to([((near[0], far[0])[i], u8(xq[:, a:e]), u8(T["ca%d" % k][:, 0:e - a]), "rc%d" % k)], 1)
        if k == 3:
            break
        rc, rs, vl, tb = T["rc%d" % k], T["rs%d" % k], T["vl%d" % k], T["tab%d" % k]
        zt, zq, zs, xn, yn = T["zt%d" % k], T["zq%d" % k], T["zs%d" % k], T["xt%d" % (k + 1)], T["xb%d" % ((k + 1) % 2)]
        back = backs[k]
        out_to([(far[1], xs[:, :], T["sa%d" % k][:, :], "rc%d" % k)], 1)
        if k == 0:
            k_hto = cp(T.hto[:, :], T.hti[:, :], ("dh", 64))
        sa, sb = [], []
        for i, (a, e) in enumerate(PARTS):
            m = [mm(bank(4 * i + d, e - a), T.uqp[:, 128 * d:128 * d + 128], T.usp[:, 128 * d:128 * d + 128], xq[:, a:e], xs[:, a:e], q0[i], k_up, k_us, psfree) for d in range(2)]
            sa.append(ts(T.sg[:, a:e], bank(4 * i, e - a), 0.0, float(C), A.is_gt, A.mult, deps=(m[0],)))
            need("se", m[1], k_bc)
            sb.append(op("se", lambda i=i, a=a, e=e: s.activation(T.sg[:, C + a:C + e], bank(4 * i + 1, e - a), AF.Sign, bias=T.bc[:, 0:1])))
        ga = tt(T.ga[:, :], T.sg[:, 0:C].indirect(T.hto[:, 0:L]), T.ramp[:, :], A.add, sa, k_hto, g_rm)
        gb = act(T.gb[:, :], T.sg[:, C:2 * C].indirect(T.hto[:, L:2 * L]), sb, k_hto)
        sca = lay(T.sc[:, 0:C], T.ga[:, :], T.fw[:, :], -K, ga, k_fw)
        scb = lay(T.sc[:, C:2 * C], T.gb[:, :], T.fw[:, :], -K, gb) if k == 0 else None
        ua = ts((T.ul if k else T.bl)[:, 0:L], T.sc[:, 15:C:16], T.cw[:, 0:1], None, A.add, deps=(sca, cw))
        psfree = psfree + sa + sb
        call = ("c%d" % k, sum(len(share(topo, c, core, 0, 1)) for c in (back[0][0], back[1][0], back[1][1])))
        msg = ("m%d" % k, len(share(topo, back[0][1], core, 0, 1)))
        dc, lg, plan = {}, {}, HOST if k else GUEST

        def unpack(b):
            i = (2, 3, 6, 7)[b]
            m = mm(bank(i, C), T.eq[:, 128 * b:128 * b + 128], T.es[:, 128 * b:128 * b + 128], rc[:, :], rs[:, :], call, k_eq, addread)
            dc[b] = act(T.ds[:, C * b:C * b + C], bank(i, C), m)

        def larger(b):
            lg[b] = tt(T.mm[:, C * b:C * b + C], T.ds[:, C * b:C * b + C].indirect(T["hq%d" % k][:, :]), xt[:, b:4 * C:4], A.max, dc[b], hq[k])

        def step(i, o, w, off, c, tok, between=None):
            r, (h, copies, picks) = [], plan[i]
            if h:
                r.append(cp(o[:, 0:16 * h], w[:, :].indirect(off[:, c:c + h]), tok))
            r.append(act(o[:, 16 * h:C], w[:, :].indirect(off[:, c + h:c + L]), tok))
            r2 = between() if between else None
            for b in picks:
                larger(b)
            for b in copies:
                unpack(b)
            return r, r2

        def lists(src, *deps):
            n = tt(T.nt[:, 0:L], src, tb[:, 2 * L:3 * L], A.mult, tab[k], *deps)
            n = tt(T.nt[:, L:2 * L], T.nt[:, 0:L], tb[:, 3 * L:4 * L], A.add, n)
            return cp(T.nu[:, :], T.nt[:, L:2 * L], n)

        def walk(ul, tok, signs):
            t, n = step(0, T.ya, T.gw, ul, 0, [tok, win[k]], signs)
            t2, _ = step(1, T.yb, T.ya, T.nu, 0, [t, n])
            c = lay(T.sp[:, :], T.yb[:, :], T.fv[:, :], T.iv[:, 0:1], t2, k_static)

            def on(e, a, w):
                return ts(T.slot[a + 32 * e:a + 32 * e + w, L * e:L * e + L], T.sp[a:a + w, 15:C:16], T.cv[a:a + w, 0:1], None, A.add, deps=(c,))
            c1 = [on(1, a, 32) for a in (0, 32, 64)]
            t, c2 = step(2, T.ya, T.yb, T.slot, L, [t2, c1], lambda: [on(2, 0, 64), on(3, 0, 32)])
            t, _ = step(3, T.yb, T.ya, T.slot, 2 * L, [t, c2])
            t, _ = step(4, T.ya, T.yb, T.slot, 3 * L, [t])
            if k == 0:
                guests(1)
                window(1, 1)
            c = lay(T.sv[:, :], T.ya[:, :], T.fv[:, :], T.iv[:, 0:1], t)
            return t, ts(vl[:, :], T.sv[:, 15:C:16], T.cv[:, 0:1], None, A.add, deps=(c,))

        if k == 0:
            ub = ts(T.bl[:, L:2 * L], T.sc[:, C + 15:2 * C:16], T.cw[:, 1:2], None, A.add, deps=(scb,))
            need("gp", ua, ub)
            out_to([(near[1], T.bl[:, :], T.br[:, :], "rm0")], 1)
            ytok = [act(xb[:, :], xt[:, :], xtok, scale=64.0)]
            e1 = ts(T.t1[:, 0:4 * L], T.eo[:, 0:8 * L:2], T.pf[:, 3:4], None, A.mult, deps=(("de", 48), g_eo, c0))
            e2 = ts(T.t1[:, 4 * L:8 * L], T.eo[:, 1:8 * L:2], T.pf[:, 1:2], None, A.mult)
            k_ec = cp(T.et[:, 4:516:4], T.idn[:, :], k_et, g_id)
            e3 = tt(tb[:, 0:2 * L], T.t1[:, 0:2 * L], T.t1[:, 4 * L:6 * L], A.add, e1, e2)
            e4 = tt(T.sel[:, 0:2 * L], T.t1[:, 2 * L:4 * L], T.t1[:, 6 * L:8 * L], A.add)
            tab[0] = cp(T.gt0[:, :], tb[:, 0:2 * L], e3)
            for i in range(2):
                window(0, i)

            def unit(b):
                return qu(T.eq[:, 128 * b:128 * b + 128], T.es[:, 128 * b:128 * b + 128], T.et[:, 4 - b:516 - b], k_ec)
            e5 = tt(T.sel[:, 2 * L:3 * L], T.sel[:, L:2 * L], T.sel[:, 0:L], A.subtract, e4)
            unit(0)
            ts(tb[:, 2 * L:3 * L], T.sel[:, 2 * L:3 * L], 0.5, None, A.mult, deps=(e5,))
            e6 = ts(T.sel[:, 3 * L:4 * L], T.sel[:, 2 * L:3 * L], T.cw[:, 1:2], 0.5, A.mult, A.mult)
            unit(1)
            tab[0] = tt(tb[:, 3 * L:4 * L], T.sel[:, 3 * L:4 * L], T.sel[:, 0:L], A.add, e6)
            need("gp", tab[0])
            out_to([(far[1], tb[:, :], T.gr[:, :], "rg")], 1)
            unit(2)
            k_eq = unit(3)
            hosts(0)
            need("sy", call)
            g.sync.dma_start(u8(T.wq[:, :]), T.wc[:, :]).then_inc(T.sem.dw, 16)
            g.sync.dma_start(T.wsc[:, :], T.ws[:, :]).then_inc(T.sem.dw, 16)
            g.sync.dma_start(T.vt[:, :], T.v[:, :]).then_inc(T.sem.dv, 16)

            def signs():
                return lists(T.nt[:, 2 * L:3 * L], ts(T.nt[:, 2 * L:3 * L], T.bb[:, L:2 * L], T.cw[:, 1:2], None, A.subtract, deps=(msg,)))
            t, k_vl = walk(T.bb, msg, signs)
            mine = vl
        else:
            def signs():
                return lists(T.sc[:, C + 15:2 * C:16], lay(T.sc[:, C:2 * C], T.gb[:, :], T.fw[:, :], -K, gb))
            t, c = walk(T.ul, ua, signs)
            need("gp", c)
            out_to([(near[1], vl[:, :], T["vr%d" % k][:, :], "rm%d" % k)], 1)
            if k == 2:
                c6 = cp(T.slot[0:16, 0:L], vl[96:112, :], c)
                t8 = act(T.yb[:, :], T.ya[:, :].indirect(T.slot[:, 0:L]), t, c6)
                need("sy", t)
                g.sync.dma_start(T.po[0:112, :], T.ya[16:128:16, :]).then_inc(T.sem.dp, 16)
                need("sy", t8)
                g.sync.dma_start(T.po[112:128, :], T.yb[0:1, :]).then_inc(T.sem.dp, 16)
                need("gp", ("dp", 32))
                out_to([(far[1], T.po[:, :], T.pr[:, :], "rl")], 1)
            k_vl, mine = msg, T["rv%d" % k]
        for b in range(4):
            if b not in dc:
                unpack(b)
        for b in range(4):
            if b not in lg:
                larger(b)
        if k == 1:
            for i in range(2):
                window(2, i)
        lg = list(lg.values())
        psfree = psfree + list(dc.values())
        zc = [[], []]

        def mosaic(i, b, e):
            a, z = PARTS[i]
            o, w = zt[:, 4 * a + b:4 * z:4], T.mm[:, C * b:C * b + C].indirect(mine[:, a // 16:z // 16])
            zc[i].append(cp(o, w, k_vl, lg[b]) if e == "ve" else act(o, w, k_vl, lg[b]))

        xtok, ynew = [[], []], []

        def layer(i):
            a, z = PARTS[i]
            qz = qu(zq[:, a:z], zs[:, a:z], zt[:, 4 * a:4 * z], zc[i])
            return [mm(bank(4 * i + b, z - a), T.wq[:, 128 * b:128 * b + 128], T.wsc[:, 128 * b:128 * b + 128], zq[:, a:z], zs[:, a:z], qz, ("dw", 32), psfree) for b in range(4)]

        def state(i, b, m):
            a, z = PARTS[i]
            ad = tt(yn[:, 4 * a + b:4 * z:4], bank(4 * i + b, z - a), xb[:, 4 * a + b:4 * z:4], A.add, m, ytok)
            xtok[i].append(act(xn[:, 4 * a + b:4 * z:4], yn[:, 4 * a + b:4 * z:4], ad, scale=2.0 ** -6))
            ynew.append(ad)
        for i, b, e in ((0, 2, "ve"), (0, 0, "se"), (0, 3, "ve"), (0, 1, "se"), (1, 0, "se"), (1, 1, "se"), (1, 2, "se")):
            mosaic(i, b, e)
        ma = layer(0)
        mosaic(1, 3, "ve")
        for b in range(2):
            state(0, b, ma[b])
        mb = layer(1)
        for b in range(2, 4):
            state(0, b, ma[b])
        for b in range(4):
            state(1, b, mb[b])
        ytok = addread = ynew
        psfree = psfree + ynew
        if k == 0:
            window(1, 0)
            hosts(1)
            guests(2)
            hosts(2)
        if k == 1:
            k_v = qu(T.vq[:, :], T.vs[:, :], T.vt[:, :], ("dv", 16))

    do = [0]

    def store(e, out, a, *deps):
        need(e, *deps)
        queue[e].dma_start(out, a).then_inc(T.sem.do, 16)
        do[0] += 16
    yc = []
    for i, (a, e) in enumerate(PARTS):
        m = mm(bank(4 * i, e - a), T.vq[:, :], T.vs[:, :], T.xq3[:, a:e], T.xs3[:, a:e], q0[i], k_v, psfree)
        yc.append(cp(T.yt[:, a:e], bank(4 * i, e - a), m))
    for i, (a, e) in enumerate(PARTS):
        store("sy", T.oc[:, 4 * a:4 * e], u8(T.xq3[:, a:e]), q0[i])
    for b in range(4):
        store(("sy", "se")[b % 2], T.osc[4 * b:4 * b + 4, :], T.xs3[32 * b:32 * b + 4, :], q0)
    for i, (a, e) in enumerate(PARTS):
        store(("se", "sy")[i], T.y[:, a:e], T.yt[:, a:e], yc[i])
    store("se", T.pl[:, :], T.pn[:, :], ("pl", len(share(topo, backs[2][1][1], core, 0, 1))))
    g.sync.wait_ge(T.sem.do, do[0])
    for e in ("ve", "se", "pe", "gp"):
        need("gp", (e, count[e]))
    g.wait_ge(T.sem.sent, sent[0])
